import numpy as np
import ml_dtypes


def mxq(x, axis, fmt="e4m3"):
    dtype, down = {"e4m3": (ml_dtypes.float8_e4m3fn, 7), "e5m2": (ml_dtypes.float8_e5m2, 14)}[fmt]
    v = np.moveaxis(np.asarray(x, np.float32).astype(ml_dtypes.bfloat16).astype(np.float64), axis, -1)
    blocks = v.reshape(v.shape[:-1] + (-1, 32))
    amax = np.abs(blocks).max(-1, keepdims=True)
    byte = np.maximum(np.where(amax > 0, np.frexp(amax)[1] - 1 + 127, 0) - down, 1)
    scale = np.exp2(byte - 127.0)
    codes = (blocks / scale).astype(np.float32).astype(dtype).astype(np.float64)
    return np.moveaxis((codes * scale).reshape(v.shape), -1, axis)


WIDE = False


def mx_kscale(k):
    if not WIDE:
        return np.ones(k)
    levels = np.array([10, -10, 5, -5, 0])
    if k % 512:
        return np.exp2(np.random.permutation(np.resize(levels, k // 32))).repeat(32)
    a = np.empty((k // 512, 16))
    for p in range(k // 512):
        a[p, :8] = np.random.permutation(np.resize(levels, 8))
        for g in range(8):
            far = levels[np.abs(levels - a[p, g]) >= 10]
            a[p, g + 8] = far[np.random.randint(len(far))]
    return np.exp2(a.ravel()).repeat(32)


def f64(x):
    return np.asarray(x).astype(np.float64)


def striped(idx):
    return np.tile(idx.reshape(-1, 16).T, (8, 1)).astype(np.uint16)


def unstriped(offs):
    return offs[:16].T.reshape(-1).astype(np.int64)


def striped8(idx):
    return np.concatenate([x.reshape(-1, 16).T for x in idx]).astype(np.uint16)


def runs(offs, k):
    lists = np.stack([offs[16 * r : 16 * r + 16].T.reshape(-1) for r in range(8)]).astype(np.int64)
    return lists[np.arange(k) % 512 // 64]


def pack_weight(w):
    k, n = w.shape
    w = f64(np.asarray(w, np.float32).astype(ml_dtypes.bfloat16)).reshape(k // 32, 32, n)
    amax = np.abs(w).max(1)
    byte = np.clip(np.where(amax > 0, np.frexp(amax)[1] - 1 + 127 - 7, 1), 1, 254)
    scaled = (w * np.exp2(127.0 - byte)[:, None, :]).reshape(k, n).astype(np.float32)
    words = np.ascontiguousarray(scaled.reshape(k // 512, 128, 4, n).transpose(0, 1, 3, 2)).astype(ml_dtypes.float8_e4m3fn).view(np.uint8)
    return words, np.ascontiguousarray(byte.astype(np.uint8).reshape(k // 512, 16, n))


def unpack_weight(words, scales):
    g, p, n, _ = words.shape
    vals = np.ascontiguousarray(words).view(ml_dtypes.float8_e4m3fn).astype(np.float64) * np.repeat(np.exp2(scales.astype(np.float64) - 127.0), 8, axis=1)[..., None]
    return vals.transpose(0, 1, 3, 2).reshape(g * 512, n)


def relu(v):
    return np.maximum(v, 0.0)

def planes(y):
    n, m = y.shape
    v = y.astype(np.float32).astype(ml_dtypes.bfloat16).astype(np.float64).reshape(n // 32, 32, m)
    top = np.abs(v).max(1)
    byte = np.clip(np.where(top > 0, np.frexp(top)[1] - 1 + 127 - 7, 1), 1, 254)
    codes = (v * np.exp2(127.0 - byte)[:, None, :]).reshape(n, m).astype(np.float32).astype(ml_dtypes.float8_e4m3fn).view(np.uint8)
    words = codes.reshape(n // 512, 128, 4, m).transpose(0, 1, 3, 2)
    return np.ascontiguousarray(words), np.ascontiguousarray(byte.astype(np.uint8).reshape(n // 512, 16, m))


K, T, S, V, N, H = 512, 2048, 512, 256, 512, 512


def setup_inputs():
    n = np.random.standard_normal
    s = mx_kscale(K)[:, None]
    u = mx_kscale(H)
    packed_xT = pack_weight(n((K, T)) * s)
    packed_w2 = pack_weight(n((H, N)) / np.sqrt(H) / u[:, None])
    return {
        "x_words": packed_xT[0],
        "x_scales": packed_xT[1],
        "w1": (n((K, H)) / np.sqrt(K) / s * u).astype(np.float32),
        "fr1": np.repeat(np.random.uniform(0, 1, (8, V)), 64, axis=0).astype(np.float32),
        "fr2": np.repeat(np.random.uniform(0, 1, (8, V)), 64, axis=0).astype(np.float32),
        "w2_words": packed_w2[0],
        "w2_scales": packed_w2[1],
        "offs": striped(np.random.permutation(T)[:S]),
        "l1": striped8(np.stack([np.random.permutation(S)[:V] for _ in range(8)])),
        "r1": striped8(np.stack([np.random.permutation(S)[:V] for _ in range(8)])),
        "l2": striped8(np.stack([np.random.permutation(S)[:V] for _ in range(8)])),
        "r2": striped8(np.stack([np.random.permutation(S)[:V] for _ in range(8)])),
    }


def reference(x_words, x_scales, w1, fr1, fr2, w2_words, w2_scales, offs, l1, r1, l2, r2):
    xq = unpack_weight(x_words, x_scales)[:, unstriped(offs)]
    y = mxq(f64(w1), 0, "e4m3").T @ xq
    q1 = y[np.arange(H)[:, None], runs(r1, H)]
    q2 = y[np.arange(H)[:, None], runs(r2, H)]
    z = relu(np.maximum(q1 + f64(fr1) * (y[np.arange(H)[:, None], runs(l1, H)] - q1), q2 + f64(fr2) * (y[np.arange(H)[:, None], runs(l2, H)] - q2)))
    out_0 = unpack_weight(w2_words, w2_scales).T @ mxq(z, 0, "e4m3")
    return (out_0,) + planes(out_0)

@@ -1,0 +1,165 @@
+from contextlib import ExitStack
+
+import concourse.mybir as mybir
+from concourse.masks import make_identity
+
+K, T, S, V, N, H = 512, 2048, 512, 256, 512, 512
+FLOPS = 2 * K * H * S + 2 * H * N * V
+BYTES = K * T + K * T // 32 + 4 * K * H + 2 * 8 * V * 4 + H * N + H * N // 32 + 2 * 128 * (32 + 4 * 16) + 4 * N * V + N * V + N * V // 32
+
+F32 = mybir.dt.float32
+BF16 = mybir.dt.bfloat16
+I32 = mybir.dt.int32
+U32 = mybir.dt.uint32
+U16 = mybir.dt.uint16
+U8 = mybir.dt.uint8
+FP8X4 = mybir.dt.float8_e4m3fn_x4
+ALU = mybir.AluOpType
+ACT = mybir.ActivationFunctionType
+
+P = 128
+HALF = 128
+NBUF = 6
+
+
+def tile_picked_roial_relu_po_kernel(
+    tc, x_words, x_scales, w1, fr1, fr2, w2_words, w2_scales, offs, l1, r1, l2, r2, out_0, out_1, out_2
+):
+    nc = tc.nc
+    with ExitStack() as ctx:
+        keep = ctx.enter_context(tc.tile_pool(name="keep", bufs=1))
+        ring = ctx.enter_context(tc.tile_pool(name="ring", bufs=2))
+        stage = ctx.enter_context(tc.tile_pool(name="stage", bufs=1))
+        psum = ctx.enter_context(tc.psum_pool(name="psum", bufs=1))
+
+        offs_sb = keep.tile([P, S // 16], U16, name="offs_sb")
+        lists = [keep.tile([P, V // 16], U16, name=f"list{i}") for i in range(4)]
+        w1_raw = stage.tile([P, 4, H], F32, name="w1_raw", offset=0)
+        x_win = keep.tile([P, T], U32, name="x_win")
+        xs_win = keep.tile([P, T], U8, name="xs_win")
+        w2_raw = stage.tile([P, N], I32, name="w2_raw", offset=2048)
+        w2s_raw = keep.tile([P, N], U8, name="w2s_raw")
+        f = [stage.tile([P, V], F32, name=f"f{i}", offset=1024 * i) for i in range(2)]
+        g = [keep.tile([P, V], F32, name=f"g{i}") for i in range(2)]
+        ident = keep.tile([P, P], F32, name="ident")
+
+        nc.gpsimd.memset(xs_win[:].bitcast(I32), 0)
+        nc.sync.dma_start(offs_sb[:], offs)
+        nc.sync.dma_start(w1_raw[:], w1.rearrange("(p j) c -> p j c", j=4))
+        nc.sync.dma_start(lists[0][:], l1)
+        nc.sync.dma_start(lists[1][:], r1)
+        nc.sync.dma_start(x_win[:].bitcast(I32), x_words[0].rearrange("p n t -> p (n t)").bitcast(I32))
+        nc.sync.dma_start(lists[2][:], l2)
+        nc.sync.dma_start(lists[3][:], r2)
+        for q in range(4):
+            eng = nc.gpsimd if q < 2 else nc.scalar
+            eng.dma_start(xs_win[32 * q : 32 * q + 4, :].bitcast(I32), x_scales[0][4 * q : 4 * q + 4, :].bitcast(I32))
+        nc.gpsimd.memset(w2s_raw[:].bitcast(I32), 0)
+        for q in range(4):
+            nc.gpsimd.dma_start(w2s_raw[32 * q : 32 * q + 4, :].bitcast(I32), w2_scales[0][4 * q : 4 * q + 4, :].bitcast(I32))
+        make_identity(nc, ident[:])
+
+        xs_g = keep.tile([P, S], U8, name="xs_g", align_bytes=64)
+        nc.vector.tensor_copy(xs_g[:], xs_win[:].indirect(offs_sb[:]))
+
+        w1_b = keep.tile([P, 4, P, 4], BF16, name="w1_b", align_bytes=64)
+        SPLIT = 96
+        src = w1_raw[:].rearrange("p j (m t) -> p m j t", t=4)
+        dst = w1_b[:].rearrange("p t m j -> p m j t")
+        nc.vector.tensor_copy(dst[:, :SPLIT], src[:, :SPLIT])
+        nc.scalar.copy(dst[:, SPLIT:], src[:, SPLIT:])
+        nc.sync.dma_start(f[0][:], fr1.rearrange("(p t) v -> p t v", t=4)[:, 0, :])
+        nc.sync.dma_start(f[1][:], fr2.rearrange("(p t) v -> p t v", t=4)[:, 0, :])
+        nc.sync.dma_start(w2_raw[:], w2_words[0].rearrange("p n t -> p (n t)").bitcast(I32))
+        w1_c = keep.tile([P, H], U32, name="w1_c", align_bytes=64)
+        w1_s = keep.tile([P, H], U8, name="w1_s", align_bytes=64)
+        nc.vector.quantize_mx(out=w1_c[:].bitcast(FP8X4), scales=w1_s[:], in_=w1_b[:].rearrange("p t m j -> p (t m j)"))
+
+        x_g = keep.tile([P, S], U32, name="x_g", align_bytes=64)
+        for a in range(2):
+            nc.vector.tensor_copy(x_g[:, 256 * a : 256 * (a + 1)], x_win[:].indirect(offs_sb[:, 16 * a : 16 * (a + 1)]))
+
+        for i in range(2):
+            nc.scalar.activation(g[i][:], f[i][:], ACT.Copy, bias=1.0, scale=-1.0)
+
+        def product1(dst_ps, t, cols):
+            nc.tensor.matmul_mx(
+                out=dst_ps,
+                lhsT=w1_c[:, P * t : P * (t + 1)].bitcast(FP8X4),
+                lhsT_scale=w1_s[:, P * t : P * (t + 1)],
+                rhs=x_g[:, cols].bitcast(FP8X4),
+                rhs_scale=xs_g[:, cols],
+                start=True,
+                stop=True,
+            )
+
+        y = [keep.tile([P, S], F32, name=f"y{t}") for t in range(4)]
+        for a in range(2):
+            cols = slice(256 * a, 256 * (a + 1))
+            acc = psum.tile([P, 256], F32, name="acc_half", tag="acc", bufs=3)
+            product1(acc[:], 0, cols)
+            if a == 0:
+                nc.scalar.copy(y[0][:, cols], acc[:])
+            else:
+                nc.vector.tensor_copy(y[0][:, cols], acc[:])
+        w2c = keep.tile([P, 4, P], I32, name="w2c", align_bytes=64)
+        nc.vector.tensor_copy(w2c[:].rearrange("p t m -> p m t"), w2_raw[:].rearrange("p (m t) -> p m t", t=4))
+        w2s = keep.tile([P, 4, P], U8, name="w2s", align_bytes=64)
+        nc.vector.tensor_copy(w2s[:].rearrange("p t m -> p m t"), w2s_raw[:].rearrange("p (m t) -> p m t", t=4))
+        for t in range(1, 4):
+            acc = psum.tile([P, S], F32, name="acc_full", tag="acc", bufs=3)
+            product1(acc[:], t, slice(0, S))
+            nc.scalar.copy(y[t][:], acc[:])
+
+        o_c = keep.tile([P, V], I32, name="o_c", align_bytes=64)
+        o_s = keep.tile([P, V], U8, name="o_s", align_bytes=64)
+        out_rows = out_0.rearrange("(p t) v -> p t v", t=4)
+        out_words = out_1[0].rearrange("p n t -> p (n t)").bitcast(I32)
+
+        for h in range(2):
+            vs = slice(HALF * h, HALF * (h + 1))
+            ls = slice(8 * h, 8 * (h + 1))
+            zb = psum.tile([P, 2, HALF], F32, name="zb", tag="zb")
+            for u in range(2):
+                banks = []
+                for i in range(2):
+                    bank = psum.tile([P, 2, P], F32, name="bank", tag=f"s{i}", bufs=2)
+                    banks.append(bank)
+                    for e in range(2):
+                        for side in range(2):
+                            part = ring.tile([P, HALF], F32, name="part", tag="part", bufs=NBUF)
+                            share = f[i] if side == 0 else g[i]
+                            nc.vector.tensor_tensor(part[:], y[2 * u + e][:].indirect(lists[2 * i + side][:, ls]), share[:, vs], ALU.mult)
+                            nc.tensor.matmul(bank[:, e, :], part[:], ident[:], start=(side == 0), stop=(side == 1), is_transpose=True)
+                    if i == 0:
+                        first = ring.tile([P, P, 2], F32, name="first")
+                        nc.scalar.activation(first[:], bank[:].rearrange("v e p -> v p e"), ACT.Relu)
+                zt = ring.tile([P, P, 2], BF16, name="zt")
+                nc.vector.tensor_tensor(zt[:], banks[1][:].rearrange("v e p -> v p e"), first[:], ALU.max)
+                nc.tensor.transpose(zb[:, u, :], zt[:].rearrange("v p e -> v (p e)").bitcast(F32), ident[:])
+            z_b = ring.tile([P, HALF * 4], BF16, name="z_b", align_bytes=64)
+            nc.scalar.copy(z_b[:].bitcast(F32).rearrange("p (v u) -> p v u", u=2), zb[:].rearrange("p u v -> p v u"))
+            z_c = ring.tile([P, HALF], U32, name="z_c", align_bytes=64)
+            z_s = ring.tile([P, HALF], U8, name="z_s", align_bytes=64)
+            nc.vector.quantize_mx(out=z_c[:].bitcast(FP8X4), scales=z_s[:], in_=z_b[:])
+            acc = psum.tile([P, 4, HALF], F32, name="acc_out", tag="acc", bufs=3)
+            for t in range(4):
+                nc.tensor.matmul_mx(
+                    out=acc[:, t, :],
+                    lhsT=w2c[:, t, :].bitcast(FP8X4),
+                    lhsT_scale=w2s[:, t, :],
+                    rhs=z_c[:].bitcast(FP8X4),
+                    rhs_scale=z_s[:],
+                    start=True,
+                    stop=True,
+                )
+            o_b = ring.tile([P, HALF, 4], BF16, name="o_b", align_bytes=64)
+            o_f = ring.tile([P, 4, HALF], F32, name="o_f")
+            nc.scalar.copy(o_b[:], acc[:].rearrange("p t v -> p v t"))
+            nc.scalar.copy(o_f[:], acc[:])
+            nc.vector.quantize_mx(out=o_c[:, vs].bitcast(FP8X4), scales=o_s[:, vs], in_=o_b[:].rearrange("p v t -> p (v t)"))
+            nc.sync.dma_start(out_rows[:, :, vs], o_f[:])
+            nc.sync.dma_start(out_words[:, vs], o_c[:, vs])
+        for q in range(4):
+            eng = nc.sync if q % 2 == 0 else nc.scalar
+            eng.dma_start(out_2[0][4 * q : 4 * q + 4, :].bitcast(I32), o_s[32 * q : 32 * q + 4, :].bitcast(I32))

@@ -19,7 +19,7 @@ ACT = mybir.ActivationFunctionType
 
 P = 128
 HALF = 128
-NBUF = 6
+SPLIT = 48
 
 
 def tile_picked_roial_relu_po_kernel(
@@ -28,50 +28,63 @@ def tile_picked_roial_relu_po_kernel(
     nc = tc.nc
     with ExitStack() as ctx:
         keep = ctx.enter_context(tc.tile_pool(name="keep", bufs=1))
-        ring = ctx.enter_context(tc.tile_pool(name="ring", bufs=2))
         stage = ctx.enter_context(tc.tile_pool(name="stage", bufs=1))
+        work = ctx.enter_context(tc.tile_pool(name="work", bufs=1))
         psum = ctx.enter_context(tc.psum_pool(name="psum", bufs=1))
 
         offs_sb = keep.tile([P, S // 16], U16, name="offs_sb")
         lists = [keep.tile([P, V // 16], U16, name=f"list{i}") for i in range(4)]
+        ident_draft = stage.tile([P, P], F32, name="ident_draft", offset=9216 - 256)
+        x_win = stage.tile([P, T], U32, name="x_win", offset=9216)
+        xs_win = stage.tile([P, T], U8, name="xs_win", offset=17408)
         w1_raw = stage.tile([P, 4, H], F32, name="w1_raw", offset=0)
-        x_win = keep.tile([P, T], U32, name="x_win")
-        xs_win = keep.tile([P, T], U8, name="xs_win")
+        f = [stage.tile([P, V], F32, name=f"f{i}", offset=8192 * (1 - i)) for i in range(2)]
         w2_raw = stage.tile([P, N], I32, name="w2_raw", offset=2048)
         w2s_raw = keep.tile([P, N], U8, name="w2s_raw")
-        f = [stage.tile([P, V], F32, name=f"f{i}", offset=1024 * i) for i in range(2)]
         g = [keep.tile([P, V], F32, name=f"g{i}") for i in range(2)]
         ident = keep.tile([P, P], F32, name="ident")
 
-        nc.gpsimd.memset(xs_win[:].bitcast(I32), 0)
+        def load_x_scales(eng):
+            for q in range(4):
+                eng.dma_start(xs_win[32 * q : 32 * q + 4, :].bitcast(I32), x_scales[0][4 * q : 4 * q + 4, :].bitcast(I32))
+
+        def load_list(i):
+            nc.sync.dma_start(lists[i][:], (l1, r1, l2, r2)[i])
+
+        def load_w1():
+            nc.sync.dma_start(w1_raw[:], w1.rearrange("(p j) c -> p j c", j=4))
+
+        def load_x():
+            nc.sync.dma_start(x_win[:].bitcast(I32), x_words[0].rearrange("p n t -> p (n t)").bitcast(I32))
+
+        nc.vector.memset(xs_win[:].bitcast(I32), 0)
         nc.sync.dma_start(offs_sb[:], offs)
-        nc.sync.dma_start(w1_raw[:], w1.rearrange("(p j) c -> p j c", j=4))
-        nc.sync.dma_start(lists[0][:], l1)
-        nc.sync.dma_start(lists[1][:], r1)
-        nc.sync.dma_start(x_win[:].bitcast(I32), x_words[0].rearrange("p n t -> p (n t)").bitcast(I32))
-        nc.sync.dma_start(lists[2][:], l2)
-        nc.sync.dma_start(lists[3][:], r2)
+        load_list(0)
+        load_list(1)
+        load_w1()
+        load_list(2)
+        load_list(3)
+        load_x_scales(nc.sync)
+        nc.vector.memset(ident_draft[:], 0.0)
+        nc.vector.tensor_copy(ident[:], ident_draft[:])
+        make_identity(nc, ident[:], nomemset=True)
+        load_x()
+        nc.sync.dma_start(f[0][:], fr1.rearrange("(p t) v -> p t v", t=4)[:, 0, :])
+        nc.vector.memset(w2s_raw[:].bitcast(I32), 0)
         for q in range(4):
-            eng = nc.gpsimd if q < 2 else nc.scalar
-            eng.dma_start(xs_win[32 * q : 32 * q + 4, :].bitcast(I32), x_scales[0][4 * q : 4 * q + 4, :].bitcast(I32))
-        nc.gpsimd.memset(w2s_raw[:].bitcast(I32), 0)
-        for q in range(4):
-            nc.gpsimd.dma_start(w2s_raw[32 * q : 32 * q + 4, :].bitcast(I32), w2_scales[0][4 * q : 4 * q + 4, :].bitcast(I32))
-        make_identity(nc, ident[:])
+            nc.sync.dma_start(w2s_raw[32 * q : 32 * q + 4, :].bitcast(I32), w2_scales[0][4 * q : 4 * q + 4, :].bitcast(I32))
 
         xs_g = keep.tile([P, S], U8, name="xs_g", align_bytes=64)
         nc.vector.tensor_copy(xs_g[:], xs_win[:].indirect(offs_sb[:]))
 
         w1_b = keep.tile([P, 4, P, 4], BF16, name="w1_b", align_bytes=64)
-        SPLIT = 96
         src = w1_raw[:].rearrange("p j (m t) -> p m j t", t=4)
         dst = w1_b[:].rearrange("p t m j -> p m j t")
         nc.vector.tensor_copy(dst[:, :SPLIT], src[:, :SPLIT])
         nc.scalar.copy(dst[:, SPLIT:], src[:, SPLIT:])
-        nc.sync.dma_start(f[0][:], fr1.rearrange("(p t) v -> p t v", t=4)[:, 0, :])
         nc.sync.dma_start(f[1][:], fr2.rearrange("(p t) v -> p t v", t=4)[:, 0, :])
         nc.sync.dma_start(w2_raw[:], w2_words[0].rearrange("p n t -> p (n t)").bitcast(I32))
-        w1_c = keep.tile([P, H], U32, name="w1_c", align_bytes=64)
+        w1_c = stage.tile([P, H], U32, name="w1_c", align_bytes=64, offset=17408)
         w1_s = keep.tile([P, H], U8, name="w1_s", align_bytes=64)
         nc.vector.quantize_mx(out=w1_c[:].bitcast(FP8X4), scales=w1_s[:], in_=w1_b[:].rearrange("p t m j -> p (t m j)"))
 
@@ -79,8 +92,10 @@ def tile_picked_roial_relu_po_kernel(
         for a in range(2):
             nc.vector.tensor_copy(x_g[:, 256 * a : 256 * (a + 1)], x_win[:].indirect(offs_sb[:, 16 * a : 16 * (a + 1)]))
 
-        for i in range(2):
-            nc.scalar.activation(g[i][:], f[i][:], ACT.Copy, bias=1.0, scale=-1.0)
+        w2s = stage.tile([P, 4, P], U8, name="w2s", align_bytes=64, offset=9216)
+        nc.vector.tensor_copy(w2s[:], w2s_raw[:].rearrange("p (m t) -> p t m", t=4))
+        nc.gpsimd.tensor_scalar(g[0][:], f[0][:], -1.0, 1.0, ALU.mult, ALU.add)
+        nc.scalar.activation(g[1][:], f[1][:], ACT.Copy, bias=1.0, scale=-1.0)
 
         def product1(dst_ps, t, cols):
             nc.tensor.matmul_mx(
@@ -93,21 +108,17 @@ def tile_picked_roial_relu_po_kernel(
                 stop=True,
             )
 
-        y = [keep.tile([P, S], F32, name=f"y{t}") for t in range(4)]
+        y = [work.tile([P, S], F32, name=f"y{t}", offset=16384 + 2048 * t) for t in range(4)]
         for a in range(2):
             cols = slice(256 * a, 256 * (a + 1))
-            acc = psum.tile([P, 256], F32, name="acc_half", tag="acc", bufs=3)
+            acc = psum.tile([P, 256], F32, name="acc_half", tag="acc", bufs=2)
             product1(acc[:], 0, cols)
             if a == 0:
                 nc.scalar.copy(y[0][:, cols], acc[:])
             else:
                 nc.vector.tensor_copy(y[0][:, cols], acc[:])
-        w2c = keep.tile([P, 4, P], I32, name="w2c", align_bytes=64)
-        nc.vector.tensor_copy(w2c[:].rearrange("p t m -> p m t"), w2_raw[:].rearrange("p (m t) -> p m t", t=4))
-        w2s = keep.tile([P, 4, P], U8, name="w2s", align_bytes=64)
-        nc.vector.tensor_copy(w2s[:].rearrange("p t m -> p m t"), w2s_raw[:].rearrange("p (m t) -> p m t", t=4))
         for t in range(1, 4):
-            acc = psum.tile([P, S], F32, name="acc_full", tag="acc", bufs=3)
+            acc = psum.tile([P, S], F32, name="acc_full", tag="acc", bufs=2)
             product1(acc[:], t, slice(0, S))
             nc.scalar.copy(y[t][:], acc[:])
 
@@ -116,33 +127,49 @@ def tile_picked_roial_relu_po_kernel(
         out_rows = out_0.rearrange("(p t) v -> p t v", t=4)
         out_words = out_1[0].rearrange("p n t -> p (n t)").bitcast(I32)
 
+        def slot(n):
+            return 1024 * n
+
+        def gathers(u, i):
+            if (u, i) == (1, 1):
+                banks = [psum.tile([P, 2, P], F32, name=f"bank_last{h}", tag="acc", bufs=2) for h in range(2)]
+            else:
+                banks = [psum.tile([P, 2, P], F32, name=f"bank{i}{h}", tag=f"s{i}{h}") for h in range(2)]
+            for e in range(2):
+                for side in range(2):
+                    n = 8 * u + 4 * i + 2 * e + side
+                    part = work.tile([P, V], F32, name=f"part{n}", offset=slot(n))
+                    share = f[i] if side == 0 else g[i]
+                    nc.vector.tensor_tensor(part[:], y[2 * u + e][:].indirect(lists[2 * i + side][:]), share[:], ALU.mult)
+                    for h in range(2):
+                        nc.tensor.matmul(banks[h][:, e, :], part[:, HALF * h : HALF * (h + 1)], ident[:], start=(side == 0), stop=(side == 1), is_transpose=True)
+            return banks
+
+        zb = [psum.tile([P, 2, HALF], F32, name=f"zb{h}", tag=f"zb{h}") for h in range(2)]
+        first, second = {}, {}
+        for u in range(2):
+            banks = gathers(u, 0)
+            for h in range(2):
+                first[u, h] = work.tile([P, P, 2], F32, name=f"first{u}{h}", offset=24576 + 1024 * (2 * u + h))
+                nc.scalar.activation(first[u, h][:], banks[h][:].rearrange("v e p -> v p e"), ACT.Relu)
+            second[u] = gathers(u, 1)
+        for u in range(2):
+            for h in range(2):
+                zt = work.tile([P, P, 2], BF16, name=f"zt{u}{h}", offset=16384 + 2048 * 3 + 512 * (2 * u + h))
+                nc.vector.tensor_tensor(zt[:], second[u][h][:].rearrange("v e p -> v p e"), first[u, h][:], ALU.max)
+                nc.tensor.transpose(zb[h][:, u, :], zt[:].rearrange("v p e -> v (p e)").bitcast(F32), ident[:])
+        w2c = work.tile([P, 4, P], I32, name="w2c", align_bytes=64, offset=24576 + 2048)
+        nc.vector.tensor_copy(w2c[:].rearrange("p t m -> p m t"), w2_raw[:].rearrange("p (m t) -> p m t", t=4))
+
+        accs = []
         for h in range(2):
-            vs = slice(HALF * h, HALF * (h + 1))
-            ls = slice(8 * h, 8 * (h + 1))
-            zb = psum.tile([P, 2, HALF], F32, name="zb", tag="zb")
-            for u in range(2):
-                banks = []
-                for i in range(2):
-                    bank = psum.tile([P, 2, P], F32, name="bank", tag=f"s{i}", bufs=2)
-                    banks.append(bank)
-                    for e in range(2):
-                        for side in range(2):
-                            part = ring.tile([P, HALF], F32, name="part", tag="part", bufs=NBUF)
-                            share = f[i] if side == 0 else g[i]
-                            nc.vector.tensor_tensor(part[:], y[2 * u + e][:].indirect(lists[2 * i + side][:, ls]), share[:, vs], ALU.mult)
-                            nc.tensor.matmul(bank[:, e, :], part[:], ident[:], start=(side == 0), stop=(side == 1), is_transpose=True)
-                    if i == 0:
-                        first = ring.tile([P, P, 2], F32, name="first")
-                        nc.scalar.activation(first[:], bank[:].rearrange("v e p -> v p e"), ACT.Relu)
-                zt = ring.tile([P, P, 2], BF16, name="zt")
-                nc.vector.tensor_tensor(zt[:], banks[1][:].rearrange("v e p -> v p e"), first[:], ALU.max)
-                nc.tensor.transpose(zb[:, u, :], zt[:].rearrange("v p e -> v (p e)").bitcast(F32), ident[:])
-            z_b = ring.tile([P, HALF * 4], BF16, name="z_b", align_bytes=64)
-            nc.scalar.copy(z_b[:].bitcast(F32).rearrange("p (v u) -> p v u", u=2), zb[:].rearrange("p u v -> p v u"))
-            z_c = ring.tile([P, HALF], U32, name="z_c", align_bytes=64)
-            z_s = ring.tile([P, HALF], U8, name="z_s", align_bytes=64)
+            z_b = keep.tile([P, HALF * 4], BF16, name=f"z_b{h}", align_bytes=64)
+            nc.scalar.copy(z_b[:].bitcast(F32).rearrange("p (v u) -> p v u", u=2), zb[h][:].rearrange("p u v -> p v u"))
+            z_c = keep.tile([P, HALF], U32, name=f"z_c{h}", align_bytes=64)
+            z_s = keep.tile([P, HALF], U8, name=f"z_s{h}", align_bytes=64)
             nc.vector.quantize_mx(out=z_c[:].bitcast(FP8X4), scales=z_s[:], in_=z_b[:])
-            acc = psum.tile([P, 4, HALF], F32, name="acc_out", tag="acc", bufs=3)
+            acc = psum.tile([P, 4, HALF], F32, name=f"acc_out{h}", tag=f"s0{h}")
+            accs.append(acc)
             for t in range(4):
                 nc.tensor.matmul_mx(
                     out=acc[:, t, :],
@@ -153,13 +180,19 @@ def tile_picked_roial_relu_po_kernel(
                     start=True,
                     stop=True,
                 )
-            o_b = ring.tile([P, HALF, 4], BF16, name="o_b", align_bytes=64)
-            o_f = ring.tile([P, 4, HALF], F32, name="o_f")
-            nc.scalar.copy(o_b[:], acc[:].rearrange("p t v -> p v t"))
-            nc.scalar.copy(o_f[:], acc[:])
-            nc.vector.quantize_mx(out=o_c[:, vs].bitcast(FP8X4), scales=o_s[:, vs], in_=o_b[:].rearrange("p v t -> p (v t)"))
-            nc.sync.dma_start(out_rows[:, :, vs], o_f[:])
-            nc.sync.dma_start(out_words[:, vs], o_c[:, vs])
+        o_b = keep.tile([P, V, 4], BF16, name="o_b", align_bytes=64)
+        for h in range(2):
+            nc.scalar.copy(o_b[:, HALF * h : HALF * (h + 1), :], accs[h][:].rearrange("p t v -> p v t"))
+        for h in range(2):
+            o_f = keep.tile([P, 4, HALF], F32, name=f"o_f{h}")
+            if h == 0:
+                nc.vector.tensor_copy(o_f[:], accs[h][:])
+                nc.sync.dma_start(out_rows[:, :, HALF * h : HALF * (h + 1)], o_f[:])
+            else:
+                nc.scalar.copy(o_f[:], accs[h][:])
+                nc.scalar.dma_start(out_rows[:, :, HALF * h : HALF * (h + 1)], o_f[:])
+        nc.vector.quantize_mx(out=o_c[:].bitcast(FP8X4), scales=o_s[:], in_=o_b[:].rearrange("p v t -> p (v t)"))
+        nc.sync.dma_start(out_words, o_c[:])
         for q in range(4):
-            eng = nc.sync if q % 2 == 0 else nc.scalar
+            eng = nc.sync if q < 2 else nc.scalar
             eng.dma_start(out_2[0][4 * q : 4 * q + 4, :].bitcast(I32), o_s[32 * q : 32 * q + 4, :].bitcast(I32))

@@ -19,7 +19,7 @@ ACT = mybir.ActivationFunctionType
 
 P = 128
 HALF = 128
-SPLIT = 48
+SPLIT = 64
 
 
 def tile_picked_roial_relu_po_kernel(
@@ -41,7 +41,7 @@ def tile_picked_roial_relu_po_kernel(
         f = [stage.tile([P, V], F32, name=f"f{i}", offset=8192 * (1 - i)) for i in range(2)]
         w2_raw = stage.tile([P, N], I32, name="w2_raw", offset=2048)
         w2s_raw = keep.tile([P, N], U8, name="w2s_raw")
-        g = [keep.tile([P, V], F32, name=f"g{i}") for i in range(2)]
+        g = [keep.tile([P, V], F32, name="g0"), stage.tile([P, V], F32, name="g1", offset=9216 + 1024)]
         ident = keep.tile([P, P], F32, name="ident")
 
         def load_x_scales(eng):
@@ -92,8 +92,9 @@ def tile_picked_roial_relu_po_kernel(
         for a in range(2):
             nc.vector.tensor_copy(x_g[:, 256 * a : 256 * (a + 1)], x_win[:].indirect(offs_sb[:, 16 * a : 16 * (a + 1)]))
 
-        w2s = stage.tile([P, 4, P], U8, name="w2s", align_bytes=64, offset=9216)
-        nc.vector.tensor_copy(w2s[:], w2s_raw[:].rearrange("p (m t) -> p t m", t=4))
+        w2s_dealt = w2s_raw[:].rearrange("p (m t) -> p t m", t=4)
+        w2s = [stage.tile([P, 2, P], U8, name=f"w2s{u}", align_bytes=64, offset=(9216, 2048)[u]) for u in range(2)]
+        nc.vector.tensor_copy(w2s[0][:], w2s_dealt[:, 0:2])
         nc.gpsimd.tensor_scalar(g[0][:], f[0][:], -1.0, 1.0, ALU.mult, ALU.add)
         nc.scalar.activation(g[1][:], f[1][:], ACT.Copy, bias=1.0, scale=-1.0)
 
@@ -118,7 +119,10 @@ def tile_picked_roial_relu_po_kernel(
             else:
                 nc.vector.tensor_copy(y[0][:, cols], acc[:])
         for t in range(1, 4):
-            acc = psum.tile([P, S], F32, name="acc_full", tag="acc", bufs=2)
+            if t < 3:
+                acc = psum.tile([P, S], F32, name="acc_full", tag=f"zb{t - 1}")
+            else:
+                acc = psum.tile([P, S], F32, name="acc_full", tag="acc", bufs=2)
             product1(acc[:], t, slice(0, S))
             nc.scalar.copy(y[t][:], acc[:])
 
@@ -131,10 +135,7 @@ def tile_picked_roial_relu_po_kernel(
             return 1024 * n
 
         def gathers(u, i):
-            if (u, i) == (1, 1):
-                banks = [psum.tile([P, 2, P], F32, name=f"bank_last{h}", tag="acc", bufs=2) for h in range(2)]
-            else:
-                banks = [psum.tile([P, 2, P], F32, name=f"bank{i}{h}", tag=f"s{i}{h}") for h in range(2)]
+            banks = [psum.tile([P, 2, P], F32, name=f"bank{i}{h}", tag=f"s{i}{h}") for h in range(2)]
             for e in range(2):
                 for side in range(2):
                     n = 8 * u + 4 * i + 2 * e + side
@@ -146,20 +147,30 @@ def tile_picked_roial_relu_po_kernel(
             return banks
 
         zb = [psum.tile([P, 2, HALF], F32, name=f"zb{h}", tag=f"zb{h}") for h in range(2)]
-        first, second = {}, {}
-        for u in range(2):
-            banks = gathers(u, 0)
+        def relu_out(banks, name, offset):
+            tile = work.tile([P, 2, P, 2], BF16, name=name, offset=offset)
             for h in range(2):
-                first[u, h] = work.tile([P, P, 2], F32, name=f"first{u}{h}", offset=24576 + 1024 * (2 * u + h))
-                nc.scalar.activation(first[u, h][:], banks[h][:].rearrange("v e p -> v p e"), ACT.Relu)
-            second[u] = gathers(u, 1)
-        for u in range(2):
-            for h in range(2):
-                zt = work.tile([P, P, 2], BF16, name=f"zt{u}{h}", offset=16384 + 2048 * 3 + 512 * (2 * u + h))
-                nc.vector.tensor_tensor(zt[:], second[u][h][:].rearrange("v e p -> v p e"), first[u, h][:], ALU.max)
-                nc.tensor.transpose(zb[h][:, u, :], zt[:].rearrange("v p e -> v (p e)").bitcast(F32), ident[:])
+                nc.scalar.activation(tile[:, h], banks[h][:].rearrange("v e p -> v p e"), ACT.Relu)
+            return tile
+
+        def turn_back(zt, u, h):
+            nc.tensor.transpose(zb[h][:, u, :], zt.rearrange("v p e -> v (p e)").bitcast(F32), ident[:])
+
+        early = [relu_out(gathers(0, i), f"early{i}", 24576 + 1024 * i) for i in range(2)]
+        first = relu_out(gathers(1, 0), "first", 24576 + 2048)
+        second = gathers(1, 1)
+        zt0 = work.tile([P, 2, P, 2], BF16, name="zt0", offset=16384 + 2048 * 3)
+        nc.vector.tensor_tensor(zt0[:], early[0][:], early[1][:], ALU.max)
+        for h in range(2):
+            turn_back(zt0[:, h], 0, h)
+        for h in range(2):
+            zt1 = keep.tile([P, P, 2], BF16, name=f"zt1{h}")
+            nc.vector.tensor_tensor(zt1[:], second[h][:].rearrange("v e p -> v p e"), first[:, h], ALU.max)
+            turn_back(zt1[:], 1, h)
         w2c = work.tile([P, 4, P], I32, name="w2c", align_bytes=64, offset=24576 + 2048)
         nc.vector.tensor_copy(w2c[:].rearrange("p t m -> p m t"), w2_raw[:].rearrange("p (m t) -> p m t", t=4))
+
+        nc.vector.tensor_copy(w2s[1][:], w2s_dealt[:, 2:4])
 
         accs = []
         for h in range(2):
@@ -168,13 +179,13 @@ def tile_picked_roial_relu_po_kernel(
             z_c = keep.tile([P, HALF], U32, name=f"z_c{h}", align_bytes=64)
             z_s = keep.tile([P, HALF], U8, name=f"z_s{h}", align_bytes=64)
             nc.vector.quantize_mx(out=z_c[:].bitcast(FP8X4), scales=z_s[:], in_=z_b[:])
-            acc = psum.tile([P, 4, HALF], F32, name=f"acc_out{h}", tag=f"s0{h}")
+            acc = psum.tile([P, 4, HALF], F32, name="acc_out", tag="acc", bufs=2)
             accs.append(acc)
             for t in range(4):
                 nc.tensor.matmul_mx(
                     out=acc[:, t, :],
                     lhsT=w2c[:, t, :].bitcast(FP8X4),
-                    lhsT_scale=w2s[:, t, :],
+                    lhsT_scale=w2s[t // 2][:, t % 2, :],
                     rhs=z_c[:].bitcast(FP8X4),
                     rhs_scale=z_s[:],
                     start=True,
@@ -189,8 +200,11 @@ def tile_picked_roial_relu_po_kernel(
                 nc.vector.tensor_copy(o_f[:], accs[h][:])
                 nc.sync.dma_start(out_rows[:, :, HALF * h : HALF * (h + 1)], o_f[:])
             else:
-                nc.scalar.copy(o_f[:], accs[h][:])
-                nc.scalar.dma_start(out_rows[:, :, HALF * h : HALF * (h + 1)], o_f[:])
+                for pair in range(2):
+                    ts = slice(2 * pair, 2 * pair + 2)
+                    nc.scalar.copy(o_f[:, ts], accs[h][:, ts])
+                    eng = nc.sync if pair == 0 else nc.scalar
+                    eng.dma_start(out_rows[:, ts, HALF * h : HALF * (h + 1)], o_f[:, ts])
         nc.vector.quantize_mx(out=o_c[:].bitcast(FP8X4), scales=o_s[:], in_=o_b[:].rearrange("p v t -> p (v t)"))
         nc.sync.dma_start(out_words, o_c[:])
         for q in range(4):

@@ -34,45 +34,34 @@ def tile_picked_roial_relu_po_kernel(
 
         offs_sb = keep.tile([P, S // 16], U16, name="offs_sb")
         lists = [keep.tile([P, V // 16], U16, name=f"list{i}") for i in range(4)]
-        ident_draft = stage.tile([P, P], F32, name="ident_draft", offset=9216 - 256)
-        x_win = stage.tile([P, T], U32, name="x_win", offset=9216)
-        xs_win = stage.tile([P, T], U8, name="xs_win", offset=17408)
-        w1_raw = stage.tile([P, 4, H], F32, name="w1_raw", offset=0)
-        f = [stage.tile([P, V], F32, name=f"f{i}", offset=8192 * (1 - i)) for i in range(2)]
-        w2_raw = stage.tile([P, N], I32, name="w2_raw", offset=2048)
-        w2s_raw = keep.tile([P, N], U8, name="w2s_raw")
-        g = [keep.tile([P, V], F32, name="g0"), stage.tile([P, V], F32, name="g1", offset=9216 + 1024)]
+        XS, X = 0, 4096
+        w1_raw = stage.tile([P, 4, H], F32, name="w1_raw", offset=X + 8192)
+        xs_win = stage.tile([P, T], U8, name="xs_win", offset=XS)
+        x_win = stage.tile([P, T], U32, name="x_win", offset=X)
+        f = stage.tile([P, 2, V], F32, name="f", offset=X - 2048)
         ident = keep.tile([P, P], F32, name="ident")
-
-        def load_x_scales(eng):
-            for q in range(4):
-                eng.dma_start(xs_win[32 * q : 32 * q + 4, :].bitcast(I32), x_scales[0][4 * q : 4 * q + 4, :].bitcast(I32))
-
-        def load_list(i):
-            nc.sync.dma_start(lists[i][:], (l1, r1, l2, r2)[i])
-
-        def load_w1():
-            nc.sync.dma_start(w1_raw[:], w1.rearrange("(p j) c -> p j c", j=4))
-
-        def load_x():
-            nc.sync.dma_start(x_win[:].bitcast(I32), x_words[0].rearrange("p n t -> p (n t)").bitcast(I32))
+        w2s_raw = keep.tile([P, N], U8, name="w2s_raw")
+        g = [keep.tile([P, V], F32, name="g0"), work.tile([P, V], F32, name="g1", offset=7168)]
 
         nc.vector.memset(xs_win[:].bitcast(I32), 0)
-        nc.sync.dma_start(offs_sb[:], offs)
-        load_list(0)
-        load_list(1)
-        load_w1()
-        load_list(2)
-        load_list(3)
-        load_x_scales(nc.sync)
-        nc.vector.memset(ident_draft[:], 0.0)
-        nc.vector.tensor_copy(ident[:], ident_draft[:])
-        make_identity(nc, ident[:], nomemset=True)
-        load_x()
-        nc.sync.dma_start(f[0][:], fr1.rearrange("(p t) v -> p t v", t=4)[:, 0, :])
-        nc.vector.memset(w2s_raw[:].bitcast(I32), 0)
+        nc.gpsimd.memset(w2s_raw[:].bitcast(I32), 0)
         for q in range(4):
-            nc.sync.dma_start(w2s_raw[32 * q : 32 * q + 4, :].bitcast(I32), w2_scales[0][4 * q : 4 * q + 4, :].bitcast(I32))
+            nc.gpsimd.dma_start(w2s_raw[32 * q : 32 * q + 4, :].bitcast(I32), w2_scales[0][4 * q : 4 * q + 4, :].bitcast(I32))
+        nc.sync.dma_start(offs_sb[:], offs)
+        nc.sync.dma_start(lists[0][:], l1)
+        nc.sync.dma_start(lists[1][:], r1)
+        nc.sync.dma_start(w1_raw[:], w1.rearrange("(p j) c -> p j c", j=4))
+        nc.sync.dma_start(lists[2][:], l2)
+        nc.sync.dma_start(lists[3][:], r2)
+        for q in range(4):
+            nc.sync.dma_start(xs_win[32 * q : 32 * q + 4, :].bitcast(I32), x_scales[0][4 * q : 4 * q + 4, :].bitcast(I32))
+        zeros = stage.tile([P, P], F32, name="zeros", offset=X - 256)
+        nc.vector.memset(zeros[:], 0.0)
+        nc.vector.tensor_copy(ident[:], zeros[:])
+        make_identity(nc, ident[:], nomemset=True)
+        nc.sync.dma_start(x_win[:].bitcast(I32), x_words[0].rearrange("p n t -> p (n t)").bitcast(I32))
+        for i in range(2):
+            nc.sync.dma_start(f[:, i, :], (fr1, fr2)[i].rearrange("(p t) v -> p t v", t=4)[:, 0, :])
 
         xs_g = keep.tile([P, S], U8, name="xs_g", align_bytes=64)
         nc.vector.tensor_copy(xs_g[:], xs_win[:].indirect(offs_sb[:]))
@@ -82,9 +71,9 @@ def tile_picked_roial_relu_po_kernel(
         dst = w1_b[:].rearrange("p t m j -> p m j t")
         nc.vector.tensor_copy(dst[:, :SPLIT], src[:, :SPLIT])
         nc.scalar.copy(dst[:, SPLIT:], src[:, SPLIT:])
-        nc.sync.dma_start(f[1][:], fr2.rearrange("(p t) v -> p t v", t=4)[:, 0, :])
+        w2_raw = stage.tile([P, N], I32, name="w2_raw", offset=X + 8192)
         nc.sync.dma_start(w2_raw[:], w2_words[0].rearrange("p n t -> p (n t)").bitcast(I32))
-        w1_c = stage.tile([P, H], U32, name="w1_c", align_bytes=64, offset=17408)
+        w1_c = keep.tile([P, H], U32, name="w1_c", align_bytes=64)
         w1_s = keep.tile([P, H], U8, name="w1_s", align_bytes=64)
         nc.vector.quantize_mx(out=w1_c[:].bitcast(FP8X4), scales=w1_s[:], in_=w1_b[:].rearrange("p t m j -> p (t m j)"))
 
@@ -92,121 +81,149 @@ def tile_picked_roial_relu_po_kernel(
         for a in range(2):
             nc.vector.tensor_copy(x_g[:, 256 * a : 256 * (a + 1)], x_win[:].indirect(offs_sb[:, 16 * a : 16 * (a + 1)]))
 
-        w2s_dealt = w2s_raw[:].rearrange("p (m t) -> p t m", t=4)
-        w2s = [stage.tile([P, 2, P], U8, name=f"w2s{u}", align_bytes=64, offset=(9216, 2048)[u]) for u in range(2)]
-        nc.vector.tensor_copy(w2s[0][:], w2s_dealt[:, 0:2])
-        nc.gpsimd.tensor_scalar(g[0][:], f[0][:], -1.0, 1.0, ALU.mult, ALU.add)
-        nc.scalar.activation(g[1][:], f[1][:], ACT.Copy, bias=1.0, scale=-1.0)
+        for i in range(2):
+            nc.gpsimd.tensor_scalar(g[i][:], f[:, i, :], -1.0, 1.0, ALU.mult, ALU.add)
 
-        def product1(dst_ps, t, cols):
-            nc.tensor.matmul_mx(
-                out=dst_ps,
-                lhsT=w1_c[:, P * t : P * (t + 1)].bitcast(FP8X4),
-                lhsT_scale=w1_s[:, P * t : P * (t + 1)],
-                rhs=x_g[:, cols].bitcast(FP8X4),
-                rhs_scale=xs_g[:, cols],
-                start=True,
-                stop=True,
-            )
-
-        y = [work.tile([P, S], F32, name=f"y{t}", offset=16384 + 2048 * t) for t in range(4)]
-        for a in range(2):
-            cols = slice(256 * a, 256 * (a + 1))
-            acc = psum.tile([P, 256], F32, name="acc_half", tag="acc", bufs=2)
-            product1(acc[:], 0, cols)
-            if a == 0:
-                nc.scalar.copy(y[0][:, cols], acc[:])
-            else:
-                nc.vector.tensor_copy(y[0][:, cols], acc[:])
-        for t in range(1, 4):
-            if t < 3:
-                acc = psum.tile([P, S], F32, name="acc_full", tag=f"zb{t - 1}")
-            else:
-                acc = psum.tile([P, S], F32, name="acc_full", tag="acc", bufs=2)
-            product1(acc[:], t, slice(0, S))
-            nc.scalar.copy(y[t][:], acc[:])
-
-        o_c = keep.tile([P, V], I32, name="o_c", align_bytes=64)
-        o_s = keep.tile([P, V], U8, name="o_s", align_bytes=64)
-        out_rows = out_0.rearrange("(p t) v -> p t v", t=4)
-        out_words = out_1[0].rearrange("p n t -> p (n t)").bitcast(I32)
-
-        def slot(n):
-            return 1024 * n
-
-        def gathers(u, i):
-            banks = [psum.tile([P, 2, P], F32, name=f"bank{i}{h}", tag=f"s{i}{h}") for h in range(2)]
-            for e in range(2):
-                for side in range(2):
-                    n = 8 * u + 4 * i + 2 * e + side
-                    part = work.tile([P, V], F32, name=f"part{n}", offset=slot(n))
-                    share = f[i] if side == 0 else g[i]
-                    nc.vector.tensor_tensor(part[:], y[2 * u + e][:].indirect(lists[2 * i + side][:]), share[:], ALU.mult)
-                    for h in range(2):
-                        nc.tensor.matmul(banks[h][:, e, :], part[:, HALF * h : HALF * (h + 1)], ident[:], start=(side == 0), stop=(side == 1), is_transpose=True)
-            return banks
-
-        zb = [psum.tile([P, 2, HALF], F32, name=f"zb{h}", tag=f"zb{h}") for h in range(2)]
-        def relu_out(banks, name, offset):
-            tile = work.tile([P, 2, P, 2], BF16, name=name, offset=offset)
-            for h in range(2):
-                nc.scalar.activation(tile[:, h], banks[h][:].rearrange("v e p -> v p e"), ACT.Relu)
-            return tile
-
-        def turn_back(zt, u, h):
-            nc.tensor.transpose(zb[h][:, u, :], zt.rearrange("v p e -> v (p e)").bitcast(F32), ident[:])
-
-        early = [relu_out(gathers(0, i), f"early{i}", 24576 + 1024 * i) for i in range(2)]
-        first = relu_out(gathers(1, 0), "first", 24576 + 2048)
-        second = gathers(1, 1)
-        zt0 = work.tile([P, 2, P, 2], BF16, name="zt0", offset=16384 + 2048 * 3)
-        nc.vector.tensor_tensor(zt0[:], early[0][:], early[1][:], ALU.max)
-        for h in range(2):
-            turn_back(zt0[:, h], 0, h)
-        for h in range(2):
-            zt1 = keep.tile([P, P, 2], BF16, name=f"zt1{h}")
-            nc.vector.tensor_tensor(zt1[:], second[h][:].rearrange("v e p -> v p e"), first[:, h], ALU.max)
-            turn_back(zt1[:], 1, h)
-        w2c = work.tile([P, 4, P], I32, name="w2c", align_bytes=64, offset=24576 + 2048)
+        w2s = stage.tile([P, 4, P], U8, name="w2s", align_bytes=64, offset=X + 4096)
+        nc.vector.tensor_copy(w2s[:], w2s_raw[:].rearrange("p (m t) -> p t m", t=4))
+        w2c = stage.tile([P, 4, P], I32, name="w2c", align_bytes=64, offset=X + 1024)
         nc.vector.tensor_copy(w2c[:].rearrange("p t m -> p m t"), w2_raw[:].rearrange("p (m t) -> p m t", t=4))
 
-        nc.vector.tensor_copy(w2s[1][:], w2s_dealt[:, 2:4])
+        def bank(tag, shape):
+            return psum.tile(shape, F32, name=tag, tag=tag)
 
-        accs = []
-        for h in range(2):
-            z_b = keep.tile([P, HALF * 4], BF16, name=f"z_b{h}", align_bytes=64)
-            nc.scalar.copy(z_b[:].bitcast(F32).rearrange("p (v u) -> p v u", u=2), zb[h][:].rearrange("p u v -> p v u"))
-            z_c = keep.tile([P, HALF], U32, name=f"z_c{h}", align_bytes=64)
-            z_s = keep.tile([P, HALF], U8, name=f"z_s{h}", align_bytes=64)
-            nc.vector.quantize_mx(out=z_c[:].bitcast(FP8X4), scales=z_s[:], in_=z_b[:])
-            acc = psum.tile([P, 4, HALF], F32, name="acc_out", tag="acc", bufs=2)
-            accs.append(acc)
-            for t in range(4):
-                nc.tensor.matmul_mx(
-                    out=acc[:, t, :],
-                    lhsT=w2c[:, t, :].bitcast(FP8X4),
-                    lhsT_scale=w2s[t // 2][:, t % 2, :],
-                    rhs=z_c[:].bitcast(FP8X4),
-                    rhs_scale=z_s[:],
-                    start=True,
-                    stop=True,
-                )
-        o_b = keep.tile([P, V, 4], BF16, name="o_b", align_bytes=64)
-        for h in range(2):
-            nc.scalar.copy(o_b[:, HALF * h : HALF * (h + 1), :], accs[h][:].rearrange("p t v -> p v t"))
-        for h in range(2):
-            o_f = keep.tile([P, 4, HALF], F32, name=f"o_f{h}")
-            if h == 0:
-                nc.vector.tensor_copy(o_f[:], accs[h][:])
-                nc.sync.dma_start(out_rows[:, :, HALF * h : HALF * (h + 1)], o_f[:])
-            else:
-                for pair in range(2):
-                    ts = slice(2 * pair, 2 * pair + 2)
-                    nc.scalar.copy(o_f[:, ts], accs[h][:, ts])
-                    eng = nc.sync if pair == 0 else nc.scalar
-                    eng.dma_start(out_rows[:, ts, HALF * h : HALF * (h + 1)], o_f[:, ts])
-        nc.vector.quantize_mx(out=o_c[:].bitcast(FP8X4), scales=o_s[:], in_=o_b[:].rearrange("p v t -> p (v t)"))
+        def product(dst_ps, codes, scales, t, rhs, rhs_scale):
+            nc.tensor.matmul_mx(out=dst_ps, lhsT=codes.bitcast(FP8X4), lhsT_scale=scales, rhs=rhs.bitcast(FP8X4), rhs_scale=rhs_scale, start=True, stop=True)
+
+        y = [keep.tile([P, S], F32, name=f"y{t}") for t in range(4)]
+        for a in range(2):
+            cols = slice(256 * a, 256 * (a + 1))
+            acc = bank(f"a{a}", [P, 256])
+            product(acc[:], w1_c[:, 0:P], w1_s[:, 0:P], 0, x_g[:, cols], xs_g[:, cols])
+            nc.scalar.copy(y[0][:, cols], acc[:])
+        for t in range(1, 4):
+            acc = bank(f"y{t}", [P, S])
+            product(acc[:], w1_c[:, P * t : P * (t + 1)], w1_s[:, P * t : P * (t + 1)], t, x_g[:], xs_g[:])
+            nc.scalar.copy(y[t][:], acc[:])
+
+        def gather(dst, t, i, side, vs):
+            share = f[:, i, vs] if side == 0 else g[i][:, vs]
+            nc.vector.tensor_tensor(dst, y[t][:].indirect(lists[2 * i + side][:, vs.start // 16 : vs.stop // 16]), share, ALU.mult)
+
+        def add_turned(dst_ps, parts):
+            for side in range(2):
+                nc.tensor.matmul(dst_ps, parts[side], ident[:], start=(side == 0), stop=(side == 1), is_transpose=True)
+
+        halves = [slice(0, HALF), slice(HALF, V)]
+        EARLY, FIRST, ZB0 = 0, 3072, 5120
+
+        early = []
+        for i in range(2):
+            sums = bank(f"s{i}", [P, 2, 2, P])
+            for e in range(2):
+                parts = [keep.tile([P, V], F32, name=f"part{i}{e}{side}") for side in range(2)]
+                for side in range(2):
+                    gather(parts[side][:], e, i, side, slice(0, V))
+                for h in range(2):
+                    add_turned(sums[:, h, e, :], [parts[side][:, halves[h]] for side in range(2)])
+            sample = work.tile([P, 2, P, 2], BF16, name=f"early{i}", offset=EARLY + 1024 * i)
+            nc.scalar.activation(sample[:], sums[:].rearrange("v h e p -> v h p e"), ACT.Relu)
+            early.append(sample)
+
+        zb = [bank("y3", [P, 2, HALF]), bank("z", [P, HALF])]
+        zt0 = keep.tile([P, 2, P, 2], BF16, name="zt0")
+
+        def first_pair_max():
+            nc.vector.tensor_tensor(zt0[:], early[0][:], early[1][:], ALU.max)
+            nc.tensor.transpose(zb[0][:, 0, :], zt0[:, 0].rearrange("v p e -> v (p e)").bitcast(F32), ident[:])
+            nc.tensor.transpose(zb[1][:], zt0[:, 1].rearrange("v p e -> v (p e)").bitcast(F32), ident[:])
+
+        sums = [bank(f"y{1 + i}", [P, 2, P]) for i in range(2)]
+        first = work.tile([P, P, 2], BF16, name="first", offset=FIRST)
+        n = 0
+        place = {7: EARLY}
+        for i in range(2):
+            for e in range(2):
+                parts = []
+                for side in range(2):
+                    if n == 7:
+                        first_pair_max()
+                    if n in place:
+                        part = work.tile([P, HALF], F32, name=f"half{n}", offset=place[n])
+                    else:
+                        part = keep.tile([P, HALF], F32, name=f"half{n}")
+                    gather(part[:], 2 + e, i, side, halves[0])
+                    parts.append(part[:])
+                    n += 1
+                add_turned(sums[i][:, e, :], parts)
+            if i == 0:
+                nc.scalar.activation(first[:], sums[0][:].rearrange("v e p -> v p e"), ACT.Relu)
+
+        z_b = [work.tile([P, HALF, 4], BF16, name="z_b0", align_bytes=64, offset=ZB0), keep.tile([P, HALF, 4], BF16, name="z_b1", align_bytes=64)]
+        z_words = [z_b[h][:].rearrange("p v t -> p (v t)").bitcast(F32).rearrange("p (v u) -> p v u", u=2) for h in range(2)]
+        nc.scalar.copy(z_words[1][:, :, 0], zb[1][:])
+
+        z_c = [keep.tile([P, HALF], U32, name="z_c0", align_bytes=64)]
+        z_s = [keep.tile([P, HALF], U8, name=f"z_s{h}", align_bytes=64) for h in range(2)]
+
+        def quantise_z(h):
+            nc.vector.quantize_mx(out=z_c[h][:].bitcast(FP8X4), scales=z_s[h][:], in_=z_b[h][:].rearrange("p v t -> p (v t)"))
+
+        left0 = work.tile([P, 2, HALF], F32, name="left0", offset=EARLY + 1024)
+        gather(left0[:, 0, :], 2, 0, 0, halves[1])
+        gather(left0[:, 1, :], 3, 0, 0, halves[1])
+        left10 = work.tile([P, HALF], F32, name="left10", offset=EARLY + 512)
+        gather(left10[:], 2, 1, 0, halves[1])
+        zt1 = keep.tile([P, P, 2], BF16, name="zt1")
+        nc.vector.tensor_tensor(zt1[:], sums[1][:].rearrange("v e p -> v p e"), first[:], ALU.max)
+        nc.tensor.transpose(zb[0][:, 1, :], zt1[:].rearrange("v p e -> v (p e)").bitcast(F32), ident[:])
+        nc.scalar.copy(z_words[0], zb[0][:].rearrange("p u v -> p v u"))
+        right0 = work.tile([P, 2, HALF], F32, name="right0", offset=FIRST - 768)
+        gather(right0[:, 0, :], 2, 0, 1, halves[1])
+        gather(right0[:, 1, :], 3, 0, 1, halves[1])
+        late = work.tile([P, 3, HALF], F32, name="late", offset=FIRST + 256)
+        gather(late[:, 0, :], 2, 1, 1, halves[1])
+        gather(late[:, 1, :], 3, 1, 0, halves[1])
+        s2 = keep.tile([P, 2, HALF], F32, name="s2")
+        nc.vector.tensor_tensor(s2[:, 0, :], left10[:], late[:, 0, :], ALU.add)
+        gather(late[:, 2, :], 3, 1, 1, halves[1])
+        s1 = work.tile([P, 2, HALF], F32, name="s1", offset=7168)
+        nc.vector.tensor_tensor(s1[:], left0[:], right0[:], ALU.add)
+        nc.vector.tensor_tensor(s2[:, 1, :], late[:, 1, :], late[:, 2, :], ALU.add)
+        nc.vector.scalar_tensor_tensor(z_b[1][:, :, 2:4], s1[:].rearrange("p e v -> p v e"), 0.0, s2[:].rearrange("p e v -> p v e"), ALU.max, ALU.max)
+        quantise_z(0)
+        z_c.append(work.tile([P, HALF], U32, name="z_c1", align_bytes=64, offset=ZB0))
+        quantise_z(1)
+
+        out_rows = out_0.rearrange("(p t) v -> p t v", t=4)
+        out_words = out_1[0].rearrange("p n t -> p (n t)").bitcast(I32)
+        o_s = keep.tile([P, V], U8, name="o_s", align_bytes=64)
+        o_c = keep.tile([P, V], I32, name="o_c", align_bytes=64)
+        o_b = [keep.tile([P, HALF, 4], BF16, name=f"o_b{h}", align_bytes=64) for h in range(2)]
+
+        def quantise_out(h):
+            nc.vector.quantize_mx(out=o_c[:, halves[h]].bitcast(FP8X4), scales=o_s[:, halves[h]], in_=o_b[h][:].rearrange("p v t -> p (v t)"))
+
+        acc = bank("s0", [P, 4, HALF])
+        for t in range(4):
+            product(acc[:, t, :], w2c[:, t, :], w2s[:, t, :], t, z_c[0][:], z_s[0][:])
+        nc.scalar.copy(o_b[0][:], acc[:].rearrange("p t v -> p v t"))
+        o_f = keep.tile([P, 4, HALF], F32, name="o_f0")
+        nc.scalar.copy(o_f[:], acc[:])
+        nc.sync.dma_start(out_rows[:, :, halves[0]], o_f[:])
+        quantise_out(0)
+
+        accs = [bank(f"a{u}", [P, 2, HALF]) for u in range(2)]
+        for t in range(4):
+            product(accs[t // 2][:, t % 2, :], w2c[:, t, :], w2s[:, t, :], t, z_c[1][:], z_s[1][:])
+        nc.scalar.copy(o_b[1][:, :, 0:2], accs[0][:].rearrange("p e v -> p v e"))
+        nc.vector.tensor_copy(o_b[1][:, :, 2:4], accs[1][:].rearrange("p e v -> p v e"))
+        quantise_out(1)
         nc.sync.dma_start(out_words, o_c[:])
+        for u in range(2):
+            o_f = keep.tile([P, 2, HALF], F32, name=f"o_f1{u}")
+            nc.scalar.copy(o_f[:], accs[u][:])
+            (nc.sync, nc.scalar)[u].dma_start(out_rows[:, 2 * u : 2 * u + 2, halves[1]], o_f[:])
         for q in range(4):
             eng = nc.sync if q < 2 else nc.scalar
             eng.dma_start(out_2[0][4 * q : 4 * q + 4, :].bitcast(I32), o_s[32 * q : 32 * q + 4, :].bitcast(I32))

@@ -19,7 +19,7 @@ ACT = mybir.ActivationFunctionType
 
 P = 128
 HALF = 128
-SPLIT = 64
+SPLIT = 96
 
 
 def tile_picked_roial_relu_po_kernel(
@@ -34,45 +34,45 @@ def tile_picked_roial_relu_po_kernel(
 
         offs_sb = keep.tile([P, S // 16], U16, name="offs_sb")
         lists = [keep.tile([P, V // 16], U16, name=f"list{i}") for i in range(4)]
-        XS, X = 0, 4096
-        w1_raw = stage.tile([P, 4, H], F32, name="w1_raw", offset=X + 8192)
-        xs_win = stage.tile([P, T], U8, name="xs_win", offset=XS)
+        W1, X, ROWS = 0, 8192, 112
+        w1_raw = stage.tile([P, 4, H], F32, name="w1_raw", offset=W1)
         x_win = stage.tile([P, T], U32, name="x_win", offset=X)
-        f = stage.tile([P, 2, V], F32, name="f", offset=X - 2048)
+        xs_win = keep.tile([P, T], U8, name="xs_win")
         ident = keep.tile([P, P], F32, name="ident")
         w2s_raw = keep.tile([P, N], U8, name="w2s_raw")
         g = [keep.tile([P, V], F32, name="g0"), work.tile([P, V], F32, name="g1", offset=7168)]
 
-        nc.vector.memset(xs_win[:].bitcast(I32), 0)
+        nc.sync.dma_start(xs_win[ROWS:, :].bitcast(I32), x_scales[0].bitcast(I32))
+        nc.sync.dma_start(offs_sb[:], offs)
+        nc.sync.dma_start(w1_raw[:], w1.rearrange("(p j) c -> p j c", j=4))
+        nc.sync.dma_start(lists[0][:], l1)
+        nc.sync.dma_start(x_win[:].bitcast(I32), x_words[0].rearrange("p n t -> p (n t)").bitcast(I32))
+        nc.sync.dma_start(lists[1][:], r1)
+        nc.sync.dma_start(lists[2][:], l2)
+        nc.sync.dma_start(lists[3][:], r2)
+        nc.vector.memset(xs_win[:ROWS, :].bitcast(I32), 0)
+        xs_g = keep.tile([P, S], U8, name="xs_g", align_bytes=64)
+        nc.vector.memset(xs_g[:].bitcast(I32), 0)
         nc.gpsimd.memset(w2s_raw[:].bitcast(I32), 0)
         for q in range(4):
             nc.gpsimd.dma_start(w2s_raw[32 * q : 32 * q + 4, :].bitcast(I32), w2_scales[0][4 * q : 4 * q + 4, :].bitcast(I32))
-        nc.sync.dma_start(offs_sb[:], offs)
-        nc.sync.dma_start(lists[0][:], l1)
-        nc.sync.dma_start(lists[1][:], r1)
-        nc.sync.dma_start(w1_raw[:], w1.rearrange("(p j) c -> p j c", j=4))
-        nc.sync.dma_start(lists[2][:], l2)
-        nc.sync.dma_start(lists[3][:], r2)
-        for q in range(4):
-            nc.sync.dma_start(xs_win[32 * q : 32 * q + 4, :].bitcast(I32), x_scales[0][4 * q : 4 * q + 4, :].bitcast(I32))
-        zeros = stage.tile([P, P], F32, name="zeros", offset=X - 256)
-        nc.vector.memset(zeros[:], 0.0)
-        nc.vector.tensor_copy(ident[:], zeros[:])
-        make_identity(nc, ident[:], nomemset=True)
-        nc.sync.dma_start(x_win[:].bitcast(I32), x_words[0].rearrange("p n t -> p (n t)").bitcast(I32))
-        for i in range(2):
-            nc.sync.dma_start(f[:, i, :], (fr1, fr2)[i].rearrange("(p t) v -> p t v", t=4)[:, 0, :])
+        make_identity(nc, ident[:])
 
-        xs_g = keep.tile([P, S], U8, name="xs_g", align_bytes=64)
-        nc.vector.tensor_copy(xs_g[:], xs_win[:].indirect(offs_sb[:]))
+        xs_rows = keep.tile([P, S], U8, name="xs_rows")
+        nc.vector.tensor_copy(xs_rows[:], xs_win[:].indirect(offs_sb[:]))
+        for q in range(4):
+            nc.sync.dma_start(xs_g[32 * q : 32 * q + 4, :].bitcast(I32), xs_rows[ROWS + 4 * q : ROWS + 4 * q + 4, :].bitcast(I32))
 
         w1_b = keep.tile([P, 4, P, 4], BF16, name="w1_b", align_bytes=64)
         src = w1_raw[:].rearrange("p j (m t) -> p m j t", t=4)
         dst = w1_b[:].rearrange("p t m j -> p m j t")
         nc.vector.tensor_copy(dst[:, :SPLIT], src[:, :SPLIT])
         nc.scalar.copy(dst[:, SPLIT:], src[:, SPLIT:])
-        w2_raw = stage.tile([P, N], I32, name="w2_raw", offset=X + 8192)
+        f = stage.tile([P, 2, V], F32, name="f", offset=W1)
+        w2_raw = stage.tile([P, N], I32, name="w2_raw", offset=W1 + 2048)
+        nc.sync.dma_start(f[:, 0, :], fr1.rearrange("(p t) v -> p t v", t=4)[:, 0, :])
         nc.sync.dma_start(w2_raw[:], w2_words[0].rearrange("p n t -> p (n t)").bitcast(I32))
+        nc.sync.dma_start(f[:, 1, :], fr2.rearrange("(p t) v -> p t v", t=4)[:, 0, :])
         w1_c = keep.tile([P, H], U32, name="w1_c", align_bytes=64)
         w1_s = keep.tile([P, H], U8, name="w1_s", align_bytes=64)
         nc.vector.quantize_mx(out=w1_c[:].bitcast(FP8X4), scales=w1_s[:], in_=w1_b[:].rearrange("p t m j -> p (t m j)"))

@@ -34,28 +34,26 @@ def tile_picked_roial_relu_po_kernel(
 
         offs_sb = keep.tile([P, S // 16], U16, name="offs_sb")
         lists = [keep.tile([P, V // 16], U16, name=f"list{i}") for i in range(4)]
-        W1, X, ROWS = 0, 8192, 112
+        W1, X, XS, W1B, ROWS = 0, 8192, 16384, 18432, 112
         w1_raw = stage.tile([P, 4, H], F32, name="w1_raw", offset=W1)
         x_win = stage.tile([P, T], U32, name="x_win", offset=X)
-        xs_win = keep.tile([P, T], U8, name="xs_win")
+        xs_win = stage.tile([P, T], U8, name="xs_win", offset=XS)
         ident = keep.tile([P, P], F32, name="ident")
         w2s_raw = keep.tile([P, N], U8, name="w2s_raw")
-        g = [keep.tile([P, V], F32, name="g0"), work.tile([P, V], F32, name="g1", offset=7168)]
 
         nc.sync.dma_start(xs_win[ROWS:, :].bitcast(I32), x_scales[0].bitcast(I32))
         nc.sync.dma_start(offs_sb[:], offs)
+        nc.sync.dma_start(w2s_raw[ROWS:, :].bitcast(I32), w2_scales[0].bitcast(I32))
         nc.sync.dma_start(w1_raw[:], w1.rearrange("(p j) c -> p j c", j=4))
         nc.sync.dma_start(lists[0][:], l1)
-        nc.sync.dma_start(x_win[:].bitcast(I32), x_words[0].rearrange("p n t -> p (n t)").bitcast(I32))
         nc.sync.dma_start(lists[1][:], r1)
         nc.sync.dma_start(lists[2][:], l2)
+        nc.sync.dma_start(x_win[:].bitcast(I32), x_words[0].rearrange("p n t -> p (n t)").bitcast(I32))
         nc.sync.dma_start(lists[3][:], r2)
         nc.vector.memset(xs_win[:ROWS, :].bitcast(I32), 0)
         xs_g = keep.tile([P, S], U8, name="xs_g", align_bytes=64)
         nc.vector.memset(xs_g[:].bitcast(I32), 0)
-        nc.gpsimd.memset(w2s_raw[:].bitcast(I32), 0)
-        for q in range(4):
-            nc.gpsimd.dma_start(w2s_raw[32 * q : 32 * q + 4, :].bitcast(I32), w2_scales[0][4 * q : 4 * q + 4, :].bitcast(I32))
+        nc.vector.memset(w2s_raw[:ROWS, :].bitcast(I32), 0)
         make_identity(nc, ident[:])
 
         xs_rows = keep.tile([P, S], U8, name="xs_rows")
@@ -63,7 +61,10 @@ def tile_picked_roial_relu_po_kernel(
         for q in range(4):
             nc.sync.dma_start(xs_g[32 * q : 32 * q + 4, :].bitcast(I32), xs_rows[ROWS + 4 * q : ROWS + 4 * q + 4, :].bitcast(I32))
 
-        w1_b = keep.tile([P, 4, P, 4], BF16, name="w1_b", align_bytes=64)
+        w2s_rows = stage.tile([P, 4, P], U8, name="w2s_rows", offset=XS)
+        nc.vector.tensor_copy(w2s_rows[:], w2s_raw[:].rearrange("p (m t) -> p t m", t=4))
+
+        w1_b = stage.tile([P, 4, P, 4], BF16, name="w1_b", align_bytes=64, offset=W1B)
         src = w1_raw[:].rearrange("p j (m t) -> p m j t", t=4)
         dst = w1_b[:].rearrange("p t m j -> p m j t")
         nc.vector.tensor_copy(dst[:, :SPLIT], src[:, :SPLIT])
@@ -77,15 +78,17 @@ def tile_picked_roial_relu_po_kernel(
         w1_s = keep.tile([P, H], U8, name="w1_s", align_bytes=64)
         nc.vector.quantize_mx(out=w1_c[:].bitcast(FP8X4), scales=w1_s[:], in_=w1_b[:].rearrange("p t m j -> p (t m j)"))
 
-        x_g = keep.tile([P, S], U32, name="x_g", align_bytes=64)
+        x_g = work.tile([P, S], U32, name="x_g", align_bytes=64, offset=7168)
         for a in range(2):
             nc.vector.tensor_copy(x_g[:, 256 * a : 256 * (a + 1)], x_win[:].indirect(offs_sb[:, 16 * a : 16 * (a + 1)]))
 
-        for i in range(2):
-            nc.gpsimd.tensor_scalar(g[i][:], f[:, i, :], -1.0, 1.0, ALU.mult, ALU.add)
+        g = [keep.tile([P, V], F32, name="g0")]
+        nc.scalar.activation(g[0][:], f[:, 0, :], ACT.Copy, bias=1.0, scale=-1.0)
 
-        w2s = stage.tile([P, 4, P], U8, name="w2s", align_bytes=64, offset=X + 4096)
-        nc.vector.tensor_copy(w2s[:], w2s_raw[:].rearrange("p (m t) -> p t m", t=4))
+        w2s = stage.tile([P, 4, P], U8, name="w2s", align_bytes=64, offset=W1B)
+        nc.gpsimd.memset(w2s[:].rearrange("p t m -> p (t m)").bitcast(I32), 0)
+        for q in range(4):
+            nc.sync.dma_start(w2s[32 * q : 32 * q + 4].rearrange("p t m -> p (t m)").bitcast(I32), w2s_rows[ROWS + 4 * q : ROWS + 4 * q + 4].rearrange("p t m -> p (t m)").bitcast(I32))
         w2c = stage.tile([P, 4, P], I32, name="w2c", align_bytes=64, offset=X + 1024)
         nc.vector.tensor_copy(w2c[:].rearrange("p t m -> p m t"), w2_raw[:].rearrange("p (m t) -> p m t", t=4))
 
@@ -101,10 +104,16 @@ def tile_picked_roial_relu_po_kernel(
             acc = bank(f"a{a}", [P, 256])
             product(acc[:], w1_c[:, 0:P], w1_s[:, 0:P], 0, x_g[:, cols], xs_g[:, cols])
             nc.scalar.copy(y[0][:, cols], acc[:])
+        rest = []
         for t in range(1, 4):
             acc = bank(f"y{t}", [P, S])
             product(acc[:], w1_c[:, P * t : P * (t + 1)], w1_s[:, P * t : P * (t + 1)], t, x_g[:], xs_g[:])
-            nc.scalar.copy(y[t][:], acc[:])
+            rest.append(acc)
+        nc.scalar.copy(y[1][:], rest[0][:])
+        g.append(work.tile([P, V], F32, name="g1", offset=7168))
+        nc.scalar.activation(g[1][:], f[:, 1, :], ACT.Copy, bias=1.0, scale=-1.0)
+        for t in range(2, 4):
+            nc.scalar.copy(y[t][:], rest[t - 1][:])
 
         def gather(dst, t, i, side, vs):
             share = f[:, i, vs] if side == 0 else g[i][:, vs]
@@ -169,30 +178,26 @@ def tile_picked_roial_relu_po_kernel(
         def quantise_z(h):
             nc.vector.quantize_mx(out=z_c[h][:].bitcast(FP8X4), scales=z_s[h][:], in_=z_b[h][:].rearrange("p v t -> p (v t)"))
 
-        left0 = work.tile([P, 2, HALF], F32, name="left0", offset=EARLY + 1024)
-        gather(left0[:, 0, :], 2, 0, 0, halves[1])
-        gather(left0[:, 1, :], 3, 0, 0, halves[1])
-        left10 = work.tile([P, HALF], F32, name="left10", offset=EARLY + 512)
-        gather(left10[:], 2, 1, 0, halves[1])
+        left0 = work.tile([P, 2, HALF], F32, name="left0", offset=EARLY + 512)
+        right0 = work.tile([P, 2, HALF], F32, name="right0", offset=EARLY + 1536)
+        for e in range(2):
+            gather(left0[:, e, :], 2 + e, 0, 0, halves[1])
+            gather(right0[:, e, :], 2 + e, 0, 1, halves[1])
         zt1 = keep.tile([P, P, 2], BF16, name="zt1")
         nc.vector.tensor_tensor(zt1[:], sums[1][:].rearrange("v e p -> v p e"), first[:], ALU.max)
         nc.tensor.transpose(zb[0][:, 1, :], zt1[:].rearrange("v p e -> v (p e)").bitcast(F32), ident[:])
         nc.scalar.copy(z_words[0], zb[0][:].rearrange("p u v -> p v u"))
-        right0 = work.tile([P, 2, HALF], F32, name="right0", offset=FIRST - 768)
-        gather(right0[:, 0, :], 2, 0, 1, halves[1])
-        gather(right0[:, 1, :], 3, 0, 1, halves[1])
-        late = work.tile([P, 3, HALF], F32, name="late", offset=FIRST + 256)
-        gather(late[:, 0, :], 2, 1, 1, halves[1])
-        gather(late[:, 1, :], 3, 1, 0, halves[1])
-        s2 = keep.tile([P, 2, HALF], F32, name="s2")
-        nc.vector.tensor_tensor(s2[:, 0, :], left10[:], late[:, 0, :], ALU.add)
-        gather(late[:, 2, :], 3, 1, 1, halves[1])
+        late = work.tile([P, 2, 2, HALF], F32, name="late", offset=FIRST)
+        for e in range(2):
+            for side in range(2):
+                gather(late[:, side, e, :], 2 + e, 1, side, halves[1])
         s1 = work.tile([P, 2, HALF], F32, name="s1", offset=7168)
         nc.vector.tensor_tensor(s1[:], left0[:], right0[:], ALU.add)
-        nc.vector.tensor_tensor(s2[:, 1, :], late[:, 1, :], late[:, 2, :], ALU.add)
-        nc.vector.scalar_tensor_tensor(z_b[1][:, :, 2:4], s1[:].rearrange("p e v -> p v e"), 0.0, s2[:].rearrange("p e v -> p v e"), ALU.max, ALU.max)
         quantise_z(0)
-        z_c.append(work.tile([P, HALF], U32, name="z_c1", align_bytes=64, offset=ZB0))
+        s2 = work.tile([P, 2, HALF], F32, name="s2", offset=ZB0)
+        nc.vector.tensor_tensor(s2[:], late[:, 0], late[:, 1], ALU.add)
+        nc.vector.scalar_tensor_tensor(z_b[1][:, :, 2:4], s1[:].rearrange("p e v -> p v e"), 0.0, s2[:].rearrange("p e v -> p v e"), ALU.max, ALU.max)
+        z_c.append(keep.tile([P, HALF], U32, name="z_c1", align_bytes=64))
         quantise_z(1)
 
         out_rows = out_0.rearrange("(p t) v -> p t v", t=4)

@@ -218,17 +218,21 @@ def tile_picked_roial_relu_po_kernel(
         nc.sync.dma_start(out_rows[:, :, halves[0]], o_f[:])
         quantise_out(0)
 
-        accs = [bank(f"a{u}", [P, 2, HALF]) for u in range(2)]
+        acc = bank("a0", [P, 4, HALF])
         for t in range(4):
-            product(accs[t // 2][:, t % 2, :], w2c[:, t, :], w2s[:, t, :], t, z_c[1][:], z_s[1][:])
-        nc.scalar.copy(o_b[1][:, :, 0:2], accs[0][:].rearrange("p e v -> p v e"))
-        nc.vector.tensor_copy(o_b[1][:, :, 2:4], accs[1][:].rearrange("p e v -> p v e"))
+            product(acc[:, t, :], w2c[:, t, :], w2s[:, t, :], t, z_c[1][:], z_s[1][:])
+        again = bank("a1", [P, 2, HALF])
+        for e in range(2):
+            product(again[:, e, :], w2c[:, 2 + e, :], w2s[:, 2 + e, :], e, z_c[1][:], z_s[1][:])
+        nc.scalar.copy(o_b[1][:], acc[:].rearrange("p t v -> p v t"))
+        o_hi = keep.tile([P, 2, HALF], F32, name="o_hi")
+        nc.vector.tensor_copy(o_hi[:], again[:])
+        nc.sync.dma_start(out_rows[:, 2:4, halves[1]], o_hi[:])
         quantise_out(1)
         nc.sync.dma_start(out_words, o_c[:])
-        for u in range(2):
-            o_f = keep.tile([P, 2, HALF], F32, name=f"o_f1{u}")
-            nc.scalar.copy(o_f[:], accs[u][:])
-            (nc.sync, nc.scalar)[u].dma_start(out_rows[:, 2 * u : 2 * u + 2, halves[1]], o_f[:])
+        o_lo = keep.tile([P, 2, HALF], F32, name="o_lo")
+        nc.scalar.copy(o_lo[:], acc[:, 0:2, :])
+        nc.scalar.dma_start(out_rows[:, 0:2, halves[1]], o_lo[:])
         for q in range(4):
             eng = nc.sync if q < 2 else nc.scalar
             eng.dma_start(out_2[0][4 * q : 4 * q + 4, :].bitcast(I32), o_s[32 * q : 32 * q + 4, :].bitcast(I32))

@@ -70,7 +70,7 @@ def tile_picked_roial_relu_po_kernel(
         nc.vector.tensor_copy(dst[:, :SPLIT], src[:, :SPLIT])
         nc.scalar.copy(dst[:, SPLIT:], src[:, SPLIT:])
         f = stage.tile([P, 2, V], F32, name="f", offset=W1)
-        w2_raw = stage.tile([P, N], I32, name="w2_raw", offset=W1 + 2048)
+        w2_raw = stage.tile([P, N], I32, name="w2_raw", offset=W1 + 6144)
         nc.sync.dma_start(f[:, 0, :], fr1.rearrange("(p t) v -> p t v", t=4)[:, 0, :])
         nc.sync.dma_start(w2_raw[:], w2_words[0].rearrange("p n t -> p (n t)").bitcast(I32))
         nc.sync.dma_start(f[:, 1, :], fr2.rearrange("(p t) v -> p t v", t=4)[:, 0, :])
@@ -89,7 +89,7 @@ def tile_picked_roial_relu_po_kernel(
         nc.gpsimd.memset(w2s[:].rearrange("p t m -> p (t m)").bitcast(I32), 0)
         for q in range(4):
             nc.sync.dma_start(w2s[32 * q : 32 * q + 4].rearrange("p t m -> p (t m)").bitcast(I32), w2s_rows[ROWS + 4 * q : ROWS + 4 * q + 4].rearrange("p t m -> p (t m)").bitcast(I32))
-        w2c = stage.tile([P, 4, P], I32, name="w2c", align_bytes=64, offset=X + 1024)
+        w2c = stage.tile([P, 4, P], I32, name="w2c", align_bytes=64, offset=X + 6144)
         nc.vector.tensor_copy(w2c[:].rearrange("p t m -> p m t"), w2_raw[:].rearrange("p (m t) -> p m t", t=4))
 
         def bank(tag, shape):
@@ -124,15 +124,16 @@ def tile_picked_roial_relu_po_kernel(
                 nc.tensor.matmul(dst_ps, parts[side], ident[:], start=(side == 0), stop=(side == 1), is_transpose=True)
 
         halves = [slice(0, HALF), slice(HALF, V)]
-        EARLY, FIRST, ZB0 = 0, 3072, 5120
+        EARLY, FIRST, ZB0, ZT1 = 0, 3072, 5632, 6656
 
         early = []
+        whole = stage.tile([P, 2, 2, 2, V], F32, name="whole", offset=W1 + 6144)
         for i in range(2):
             sums = bank(f"s{i}", [P, 2, 2, P])
             for e in range(2):
-                parts = [keep.tile([P, V], F32, name=f"part{i}{e}{side}") for side in range(2)]
+                parts = [whole[:, i, e, side, :] for side in range(2)]
                 for side in range(2):
-                    gather(parts[side][:], e, i, side, slice(0, V))
+                    gather(parts[side], e, i, side, slice(0, V))
                 for h in range(2):
                     add_turned(sums[:, h, e, :], [parts[side][:, halves[h]] for side in range(2)])
             sample = work.tile([P, 2, P, 2], BF16, name=f"early{i}", offset=EARLY + 1024 * i)
@@ -148,7 +149,7 @@ def tile_picked_roial_relu_po_kernel(
             nc.tensor.transpose(zb[1][:], zt0[:, 1].rearrange("v p e -> v (p e)").bitcast(F32), ident[:])
 
         sums = [bank(f"y{1 + i}", [P, 2, P]) for i in range(2)]
-        first = work.tile([P, P, 2], BF16, name="first", offset=FIRST)
+        first = work.tile([P, 2, P, 2], BF16, name="first", offset=FIRST)
         n = 0
         place = {7: EARLY}
         for i in range(2):
@@ -165,39 +166,45 @@ def tile_picked_roial_relu_po_kernel(
                     parts.append(part[:])
                     n += 1
                 add_turned(sums[i][:, e, :], parts)
-            if i == 0:
-                nc.scalar.activation(first[:], sums[0][:].rearrange("v e p -> v p e"), ACT.Relu)
+            nc.scalar.activation(first[:, i], sums[i][:].rearrange("v e p -> v p e"), ACT.Relu)
 
-        z_b = [work.tile([P, HALF, 4], BF16, name="z_b0", align_bytes=64, offset=ZB0), keep.tile([P, HALF, 4], BF16, name="z_b1", align_bytes=64)]
+        z_b = [work.tile([P, HALF, 4], BF16, name="z_b0", align_bytes=64, offset=ZB0), work.tile([P, HALF, 4], BF16, name="z_b1", align_bytes=64, offset=9216)]
         z_words = [z_b[h][:].rearrange("p v t -> p (v t)").bitcast(F32).rearrange("p (v u) -> p v u", u=2) for h in range(2)]
         nc.scalar.copy(z_words[1][:, :, 0], zb[1][:])
 
-        z_c = [keep.tile([P, HALF], U32, name="z_c0", align_bytes=64)]
+        z_c = []
         z_s = [keep.tile([P, HALF], U8, name=f"z_s{h}", align_bytes=64) for h in range(2)]
 
         def quantise_z(h):
             nc.vector.quantize_mx(out=z_c[h][:].bitcast(FP8X4), scales=z_s[h][:], in_=z_b[h][:].rearrange("p v t -> p (v t)"))
 
+        last_sums = bank("s1", [P, 2, P])
         left0 = work.tile([P, 2, HALF], F32, name="left0", offset=EARLY + 512)
         right0 = work.tile([P, 2, HALF], F32, name="right0", offset=EARLY + 1536)
         for e in range(2):
             gather(left0[:, e, :], 2 + e, 0, 0, halves[1])
             gather(right0[:, e, :], 2 + e, 0, 1, halves[1])
+            add_turned(last_sums[:, e, :], [left0[:, e, :], right0[:, e, :]])
         zt1 = keep.tile([P, P, 2], BF16, name="zt1")
-        nc.vector.tensor_tensor(zt1[:], sums[1][:].rearrange("v e p -> v p e"), first[:], ALU.max)
+        nc.vector.tensor_tensor(zt1[:], first[:, 0], first[:, 1], ALU.max)
         nc.tensor.transpose(zb[0][:, 1, :], zt1[:].rearrange("v p e -> v (p e)").bitcast(F32), ident[:])
+        last_first = keep.tile([P, P, 2], BF16, name="last_first")
+        nc.scalar.activation(last_first[:], last_sums[:].rearrange("v e p -> v p e"), ACT.Relu)
         nc.scalar.copy(z_words[0], zb[0][:].rearrange("p u v -> p v u"))
-        late = work.tile([P, 2, 2, HALF], F32, name="late", offset=FIRST)
-        for e in range(2):
-            for side in range(2):
-                gather(late[:, side, e, :], 2 + e, 1, side, halves[1])
-        s1 = work.tile([P, 2, HALF], F32, name="s1", offset=7168)
-        nc.vector.tensor_tensor(s1[:], left0[:], right0[:], ALU.add)
+        s1 = bank("a1", [P, HALF])
+        nc.tensor.transpose(s1[:], last_first[:].rearrange("v p e -> v (p e)").bitcast(F32), ident[:])
+        late = work.tile([P, 3, HALF], F32, name="late", offset=FIRST + 256)
+        for n in range(3):
+            gather(late[:, n, :], 2 + n // 2, 1, n % 2, halves[1])
+        last = work.tile([P, HALF], F32, name="last", offset=FIRST - 256)
+        gather(last[:], 3, 1, 1, halves[1])
+        s2 = stage.tile([P, 2, HALF], F32, name="s2", offset=W1)
+        nc.vector.tensor_tensor(s2[:, 0, :], late[:, 0, :], late[:, 1, :], ALU.add)
+        nc.vector.tensor_tensor(s2[:, 1, :], late[:, 2, :], last[:], ALU.add)
+        z_c.append(keep.tile([P, HALF], U32, name="z_c0", align_bytes=64))
         quantise_z(0)
-        s2 = work.tile([P, 2, HALF], F32, name="s2", offset=ZB0)
-        nc.vector.tensor_tensor(s2[:], late[:, 0], late[:, 1], ALU.add)
-        nc.vector.scalar_tensor_tensor(z_b[1][:, :, 2:4], s1[:].rearrange("p e v -> p v e"), 0.0, s2[:].rearrange("p e v -> p v e"), ALU.max, ALU.max)
-        z_c.append(keep.tile([P, HALF], U32, name="z_c1", align_bytes=64))
+        nc.vector.tensor_tensor(z_b[1][:, :, 2:4], s2[:].rearrange("p e v -> p v e"), s1[:].bitcast(BF16).rearrange("p (v e) -> p v e", e=2), ALU.max)
+        z_c.append(work.tile([P, HALF], U32, name="z_c1", align_bytes=64, offset=ZB0))
         quantise_z(1)
 
         out_rows = out_0.rearrange("(p t) v -> p t v", t=4)
@@ -212,9 +219,13 @@ def tile_picked_roial_relu_po_kernel(
         acc = bank("s0", [P, 4, HALF])
         for t in range(4):
             product(acc[:, t, :], w2c[:, t, :], w2s[:, t, :], t, z_c[0][:], z_s[0][:])
+        again = bank("y1", [P, 2, HALF])
+        for e in range(2):
+            product(again[:, e, :], w2c[:, 2 + e, :], w2s[:, 2 + e, :], e, z_c[0][:], z_s[0][:])
         nc.scalar.copy(o_b[0][:], acc[:].rearrange("p t v -> p v t"))
-        o_f = keep.tile([P, 4, HALF], F32, name="o_f0")
-        nc.scalar.copy(o_f[:], acc[:])
+        o_f = work.tile([P, 4, HALF], F32, name="o_f0", offset=9216)
+        nc.vector.tensor_copy(o_f[:, 2:4, :], again[:])
+        nc.scalar.copy(o_f[:, 0:2, :], acc[:, 0:2, :])
         nc.sync.dma_start(out_rows[:, :, halves[0]], o_f[:])
         quantise_out(0)
 

@@ -141,27 +141,15 @@ def tile_picked_roial_relu_po_kernel(
             early.append(sample)
 
         zb = [bank("y3", [P, 2, HALF]), bank("z", [P, HALF])]
-        zt0 = keep.tile([P, 2, P, 2], BF16, name="zt0")
-
-        def first_pair_max():
-            nc.vector.tensor_tensor(zt0[:], early[0][:], early[1][:], ALU.max)
-            nc.tensor.transpose(zb[0][:, 0, :], zt0[:, 0].rearrange("v p e -> v (p e)").bitcast(F32), ident[:])
-            nc.tensor.transpose(zb[1][:], zt0[:, 1].rearrange("v p e -> v (p e)").bitcast(F32), ident[:])
 
         sums = [bank(f"y{1 + i}", [P, 2, P]) for i in range(2)]
         first = work.tile([P, 2, P, 2], BF16, name="first", offset=FIRST)
         n = 0
-        place = {7: EARLY}
         for i in range(2):
             for e in range(2):
                 parts = []
                 for side in range(2):
-                    if n == 7:
-                        first_pair_max()
-                    if n in place:
-                        part = work.tile([P, HALF], F32, name=f"half{n}", offset=place[n])
-                    else:
-                        part = keep.tile([P, HALF], F32, name=f"half{n}")
+                    part = work.tile([P, HALF], F32, name=f"half{n}", offset=11264 + 512 * n)
                     gather(part[:], 2 + e, i, side, halves[0])
                     parts.append(part[:])
                     n += 1
@@ -170,7 +158,6 @@ def tile_picked_roial_relu_po_kernel(
 
         z_b = [work.tile([P, HALF, 4], BF16, name="z_b0", align_bytes=64, offset=ZB0), work.tile([P, HALF, 4], BF16, name="z_b1", align_bytes=64, offset=9216)]
         z_words = [z_b[h][:].rearrange("p v t -> p (v t)").bitcast(F32).rearrange("p (v u) -> p v u", u=2) for h in range(2)]
-        nc.scalar.copy(z_words[1][:, :, 0], zb[1][:])
 
         z_c = []
         z_s = [keep.tile([P, HALF], U8, name=f"z_s{h}", align_bytes=64) for h in range(2)]
@@ -179,28 +166,32 @@ def tile_picked_roial_relu_po_kernel(
             nc.vector.quantize_mx(out=z_c[h][:].bitcast(FP8X4), scales=z_s[h][:], in_=z_b[h][:].rearrange("p v t -> p (v t)"))
 
         last_sums = bank("s1", [P, 2, P])
-        left0 = work.tile([P, 2, HALF], F32, name="left0", offset=EARLY + 512)
-        right0 = work.tile([P, 2, HALF], F32, name="right0", offset=EARLY + 1536)
+        left0 = keep.tile([P, 2, HALF], F32, name="left0")
+        right0 = keep.tile([P, 2, HALF], F32, name="right0")
         for e in range(2):
             gather(left0[:, e, :], 2 + e, 0, 0, halves[1])
             gather(right0[:, e, :], 2 + e, 0, 1, halves[1])
             add_turned(last_sums[:, e, :], [left0[:, e, :], right0[:, e, :]])
         zt1 = keep.tile([P, P, 2], BF16, name="zt1")
+        zt0 = work.tile([P, 2, P, 2], BF16, name="zt0", offset=11264 + 512 * 6)
+        nc.vector.tensor_tensor(zt0[:], early[0][:], early[1][:], ALU.max)
         nc.vector.tensor_tensor(zt1[:], first[:, 0], first[:, 1], ALU.max)
+        nc.tensor.transpose(zb[0][:, 0, :], zt0[:, 0].rearrange("v p e -> v (p e)").bitcast(F32), ident[:])
         nc.tensor.transpose(zb[0][:, 1, :], zt1[:].rearrange("v p e -> v (p e)").bitcast(F32), ident[:])
         last_first = keep.tile([P, P, 2], BF16, name="last_first")
         nc.scalar.activation(last_first[:], last_sums[:].rearrange("v e p -> v p e"), ACT.Relu)
         nc.scalar.copy(z_words[0], zb[0][:].rearrange("p u v -> p v u"))
         s1 = bank("a1", [P, HALF])
         nc.tensor.transpose(s1[:], last_first[:].rearrange("v p e -> v (p e)").bitcast(F32), ident[:])
-        late = work.tile([P, 3, HALF], F32, name="late", offset=FIRST + 256)
-        for n in range(3):
-            gather(late[:, n, :], 2 + n // 2, 1, n % 2, halves[1])
-        last = work.tile([P, HALF], F32, name="last", offset=FIRST - 256)
-        gather(last[:], 3, 1, 1, halves[1])
+        nc.tensor.transpose(zb[1][:], zt0[:, 1].rearrange("v p e -> v (p e)").bitcast(F32), ident[:])
+        nc.scalar.copy(z_words[1][:, :, 0], zb[1][:])
+        late = [work.tile([P, 2, HALF], F32, name=f"late{e}", offset=(EARLY, FIRST)[e]) for e in range(2)]
+        for e in range(2):
+            for side in range(2):
+                gather(late[e][:, side, :], 2 + e, 1, side, halves[1])
         s2 = stage.tile([P, 2, HALF], F32, name="s2", offset=W1)
-        nc.vector.tensor_tensor(s2[:, 0, :], late[:, 0, :], late[:, 1, :], ALU.add)
-        nc.vector.tensor_tensor(s2[:, 1, :], late[:, 2, :], last[:], ALU.add)
+        for e in range(2):
+            nc.vector.tensor_tensor(s2[:, e, :], late[e][:, 0, :], late[e][:, 1, :], ALU.add)
         z_c.append(keep.tile([P, HALF], U32, name="z_c0", align_bytes=64))
         quantise_z(0)
         nc.vector.tensor_tensor(z_b[1][:, :, 2:4], s2[:].rearrange("p e v -> p v e"), s1[:].bitcast(BF16).rearrange("p (v e) -> p v e", e=2), ALU.max)

@@ -19,7 +19,7 @@ ACT = mybir.ActivationFunctionType
 
 P = 128
 HALF = 128
-SPLIT = 96
+SPLIT = 72
 
 
 def tile_picked_roial_relu_po_kernel(
@@ -41,9 +41,9 @@ def tile_picked_roial_relu_po_kernel(
         ident = keep.tile([P, P], F32, name="ident")
         w2s_raw = keep.tile([P, N], U8, name="w2s_raw")
 
-        nc.sync.dma_start(xs_win[ROWS:, :].bitcast(I32), x_scales[0].bitcast(I32))
+        nc.scalar.dma_start(xs_win[ROWS:, :].bitcast(I32), x_scales[0].bitcast(I32))
         nc.sync.dma_start(offs_sb[:], offs)
-        nc.sync.dma_start(w2s_raw[ROWS:, :].bitcast(I32), w2_scales[0].bitcast(I32))
+        nc.scalar.dma_start(w2s_raw[ROWS:, :].bitcast(I32), w2_scales[0].bitcast(I32))
         nc.sync.dma_start(w1_raw[:], w1.rearrange("(p j) c -> p j c", j=4))
         nc.sync.dma_start(lists[0][:], l1)
         nc.sync.dma_start(lists[1][:], r1)

@@ -34,12 +34,12 @@ def tile_picked_roial_relu_po_kernel(
 
         offs_sb = keep.tile([P, S // 16], U16, name="offs_sb")
         lists = [keep.tile([P, V // 16], U16, name=f"list{i}") for i in range(4)]
-        W1, X, XS, W1B, ROWS = 0, 8192, 16384, 18432, 112
+        W1, X, XS, W1B, HOLD, ROWS = 0, 8192, 16384, 18432, 22528, 112
         w1_raw = stage.tile([P, 4, H], F32, name="w1_raw", offset=W1)
         x_win = stage.tile([P, T], U32, name="x_win", offset=X)
         xs_win = stage.tile([P, T], U8, name="xs_win", offset=XS)
         ident = keep.tile([P, P], F32, name="ident")
-        w2s_raw = keep.tile([P, N], U8, name="w2s_raw")
+        w2s_raw = stage.tile([P, N], U8, name="w2s_raw", offset=HOLD + 2048 - 256)
 
         nc.scalar.dma_start(xs_win[ROWS:, :].bitcast(I32), x_scales[0].bitcast(I32))
         nc.sync.dma_start(offs_sb[:], offs)
@@ -69,8 +69,8 @@ def tile_picked_roial_relu_po_kernel(
         dst = w1_b[:].rearrange("p t m j -> p m j t")
         nc.vector.tensor_copy(dst[:, :SPLIT], src[:, :SPLIT])
         nc.scalar.copy(dst[:, SPLIT:], src[:, SPLIT:])
-        f = stage.tile([P, 2, V], F32, name="f", offset=W1)
-        w2_raw = stage.tile([P, N], I32, name="w2_raw", offset=W1 + 6144)
+        f = stage.tile([P, 2, V], F32, name="f", offset=HOLD)
+        w2_raw = stage.tile([P, N], I32, name="w2_raw", offset=HOLD + 2048)
         nc.sync.dma_start(f[:, 0, :], fr1.rearrange("(p t) v -> p t v", t=4)[:, 0, :])
         nc.sync.dma_start(w2_raw[:], w2_words[0].rearrange("p n t -> p (n t)").bitcast(I32))
         nc.sync.dma_start(f[:, 1, :], fr2.rearrange("(p t) v -> p t v", t=4)[:, 0, :])
@@ -86,7 +86,7 @@ def tile_picked_roial_relu_po_kernel(
         nc.scalar.activation(g[0][:], f[:, 0, :], ACT.Copy, bias=1.0, scale=-1.0)
 
         w2s = stage.tile([P, 4, P], U8, name="w2s", align_bytes=64, offset=W1B)
-        nc.gpsimd.memset(w2s[:].rearrange("p t m -> p (t m)").bitcast(I32), 0)
+        nc.vector.memset(w2s[:].rearrange("p t m -> p (t m)").bitcast(I32), 0)
         for q in range(4):
             nc.sync.dma_start(w2s[32 * q : 32 * q + 4].rearrange("p t m -> p (t m)").bitcast(I32), w2s_rows[ROWS + 4 * q : ROWS + 4 * q + 4].rearrange("p t m -> p (t m)").bitcast(I32))
         w2c = stage.tile([P, 4, P], I32, name="w2c", align_bytes=64, offset=X + 6144)
@@ -127,7 +127,7 @@ def tile_picked_roial_relu_po_kernel(
         EARLY, FIRST, ZB0, ZT1 = 0, 3072, 5632, 6656
 
         early = []
-        whole = stage.tile([P, 2, 2, 2, V], F32, name="whole", offset=W1 + 6144)
+        whole = stage.tile([P, 2, 2, 2, V], F32, name="whole", offset=HOLD + 2048)
         for i in range(2):
             sums = bank(f"s{i}", [P, 2, 2, P])
             for e in range(2):
@@ -189,7 +189,7 @@ def tile_picked_roial_relu_po_kernel(
         for e in range(2):
             for side in range(2):
                 gather(late[e][:, side, :], 2 + e, 1, side, halves[1])
-        s2 = stage.tile([P, 2, HALF], F32, name="s2", offset=W1)
+        s2 = stage.tile([P, 2, HALF], F32, name="s2", offset=HOLD)
         for e in range(2):
             nc.vector.tensor_tensor(s2[:, e, :], late[e][:, 0, :], late[e][:, 1, :], ALU.add)
         z_c.append(keep.tile([P, HALF], U32, name="z_c0", align_bytes=64))

@@ -19,7 +19,7 @@ ACT = mybir.ActivationFunctionType
 
 P = 128
 HALF = 128
-SPLIT = 72
+SPLIT = 88
 
 
 def tile_picked_roial_relu_po_kernel(
@@ -194,9 +194,12 @@ def tile_picked_roial_relu_po_kernel(
             nc.vector.tensor_tensor(s2[:, e, :], late[e][:, 0, :], late[e][:, 1, :], ALU.add)
         z_c.append(keep.tile([P, HALF], U32, name="z_c0", align_bytes=64))
         quantise_z(0)
-        nc.vector.tensor_tensor(z_b[1][:, :, 2:4], s2[:].rearrange("p e v -> p v e"), s1[:].bitcast(BF16).rearrange("p (v e) -> p v e", e=2), ALU.max)
+        quarters = [slice(0, HALF // 2), slice(HALF // 2, HALF)]
+        for vs in quarters:
+            nc.vector.tensor_tensor(z_b[1][:, vs, 2:4], s2[:, :, vs].rearrange("p e v -> p v e"), s1[:].bitcast(BF16).rearrange("p (v e) -> p v e", e=2)[:, vs], ALU.max)
         z_c.append(work.tile([P, HALF], U32, name="z_c1", align_bytes=64, offset=ZB0))
-        quantise_z(1)
+        for vs in quarters:
+            nc.vector.quantize_mx(out=z_c[1][:, vs].bitcast(FP8X4), scales=z_s[1][:, vs], in_=z_b[1][:, vs, :].rearrange("p v t -> p (v t)"))
 
         out_rows = out_0.rearrange("(p t) v -> p t v", t=4)
         out_words = out_1[0].rearrange("p n t -> p (n t)").bitcast(I32)

@@ -82,8 +82,8 @@ def tile_picked_roial_relu_po_kernel(
         for a in range(2):
             nc.vector.tensor_copy(x_g[:, 256 * a : 256 * (a + 1)], x_win[:].indirect(offs_sb[:, 16 * a : 16 * (a + 1)]))
 
-        g = [keep.tile([P, V], F32, name="g0")]
-        nc.scalar.activation(g[0][:], f[:, 0, :], ACT.Copy, bias=1.0, scale=-1.0)
+        g = keep.tile([P, V], F32, name="g")
+        nc.scalar.activation(g[:], f[:, 0, :], ACT.Copy, bias=1.0, scale=-1.0)
 
         w2s = stage.tile([P, 4, P], U8, name="w2s", align_bytes=64, offset=W1B)
         nc.vector.memset(w2s[:].rearrange("p t m -> p (t m)").bitcast(I32), 0)
@@ -101,102 +101,147 @@ def tile_picked_roial_relu_po_kernel(
         y = [keep.tile([P, S], F32, name=f"y{t}") for t in range(4)]
         for a in range(2):
             cols = slice(256 * a, 256 * (a + 1))
-            acc = bank(f"a{a}", [P, 256])
-            product(acc[:], w1_c[:, 0:P], w1_s[:, 0:P], 0, x_g[:, cols], xs_g[:, cols])
-            nc.scalar.copy(y[0][:, cols], acc[:])
+            for t in range(2):
+                acc = bank(("a0", "z", "a1", "y1")[2 * a + t], [P, 256])
+                product(acc[:], w1_c[:, P * t : P * (t + 1)], w1_s[:, P * t : P * (t + 1)], t, x_g[:, cols], xs_g[:, cols])
+                if (a, t) == (0, 1):
+                    nc.vector.tensor_copy(y[t][:, cols], acc[:])
+                else:
+                    nc.scalar.copy(y[t][:, cols], acc[:])
         rest = []
-        for t in range(1, 4):
+        for t in range(2, 4):
             acc = bank(f"y{t}", [P, S])
             product(acc[:], w1_c[:, P * t : P * (t + 1)], w1_s[:, P * t : P * (t + 1)], t, x_g[:], xs_g[:])
             rest.append(acc)
-        nc.scalar.copy(y[1][:], rest[0][:])
-        g.append(work.tile([P, V], F32, name="g1", offset=7168))
-        nc.scalar.activation(g[1][:], f[:, 1, :], ACT.Copy, bias=1.0, scale=-1.0)
-        for t in range(2, 4):
-            nc.scalar.copy(y[t][:], rest[t - 1][:])
 
-        def gather(dst, t, i, side, vs):
-            share = f[:, i, vs] if side == 0 else g[i][:, vs]
-            nc.vector.tensor_tensor(dst, y[t][:].indirect(lists[2 * i + side][:, vs.start // 16 : vs.stop // 16]), share, ALU.mult)
+        halves = [slice(0, HALF), slice(HALF, V)]
+        both = slice(0, V)
+        L1, R1, L2, R2 = range(4)
+
+        def looked_up(t, which, vs):
+            return y[t][:].indirect(lists[which][:, vs.start // 16 : vs.stop // 16])
+
+        def first_terms(dst, t, vs):
+            nc.vector.tensor_tensor(dst[:, 0, :], looked_up(t, L1, vs), f[:, 0, vs], ALU.mult)
+            nc.vector.tensor_tensor(dst[:, 1, :], looked_up(t, R1, vs), g[:, vs], ALU.mult)
+
+        def fetch(dst, t, which, vs):
+            nc.scalar.activation(dst, looked_up(t, which, vs), ACT.Copy)
 
         def add_turned(dst_ps, parts):
             for side in range(2):
                 nc.tensor.matmul(dst_ps, parts[side], ident[:], start=(side == 0), stop=(side == 1), is_transpose=True)
 
-        halves = [slice(0, HALF), slice(HALF, V)]
-        EARLY, FIRST, ZB0, ZT1 = 0, 3072, 5632, 6656
+        def leave(dst, sums):
+            nc.scalar.activation(dst, sums, ACT.Relu)
 
-        early = []
-        whole = stage.tile([P, 2, 2, 2, V], F32, name="whole", offset=HOLD + 2048)
-        for i in range(2):
-            sums = bank(f"s{i}", [P, 2, 2, P])
+        EARLY, LATE0, ZB0 = 0, 3072, 5632
+        left = [keep.tile([P, V], F32, name=f"left{t}") for t in range(2)]
+        right = [keep.tile([P, V], F32, name=f"right{t}") for t in range(2)]
+        step = [keep.tile([P, V], F32, name=f"step{t}") for t in range(2)]
+        diff = [keep.tile([P, V], F32, name=f"diff{t}") for t in range(2)]
+        left_b = [keep.tile([P, HALF], F32, name="left_b0"), work.tile([P, HALF], F32, name="left_b1", offset=LATE0)]
+        right_b = [keep.tile([P, 2, HALF], F32, name=f"right_b{h}") for h in range(2)]
+        step_b = [keep.tile([P, 2, HALF], F32, name=f"step_b{h}") for h in range(2)]
+        diff_b = [keep.tile([P, 2, HALF], F32, name=f"diff_b{h}") for h in range(2)]
+
+        def subtract(t):
+            nc.vector.tensor_tensor(diff[t][:], left[t][:], right[t][:], ALU.subtract)
+
+        def weigh(t):
+            nc.vector.tensor_tensor(step[t][:], diff[t][:], f[:, 1, :], ALU.mult)
+
+        def subtract_b(h, e):
+            lhs = left_b[h][:] if e == 0 else looked_up(3, L2, halves[h])
+            nc.vector.tensor_tensor(diff_b[h][:, e, :], lhs, right_b[h][:, e, :], ALU.subtract)
+
+        def weigh_b(h):
+            nc.vector.tensor_tensor(step_b[h][:], diff_b[h][:], f[:, 1:2, halves[h]].to_broadcast([P, 2, HALF]), ALU.mult)
+
+        whole = stage.tile([P, 2, 2, V], F32, name="whole", offset=HOLD + 2048)
+        sums_a = [bank(f"s{i}", [P, 2, 2, P]) for i in range(2)]
+        for e in range(2):
+            first_terms(whole[:, e], e, both)
+            for h in range(2):
+                add_turned(sums_a[0][:, h, e, :], [whole[:, e, side, halves[h]] for side in range(2)])
+
+        fetch(right[0][:], 0, R2, both)
+        fetch(left[0][:], 0, L2, both)
+        for t in range(2, 4):
+            nc.scalar.copy(y[t][:], rest[t - 2][:])
+        fetch(right[1][:], 1, R2, both)
+        fetch(left[1][:], 1, L2, both)
+        for h in range(2):
+            fetch(right_b[h][:, 0, :], 2, R2, halves[h])
+            fetch(left_b[h][:], 2, L2, halves[h])
+            fetch(right_b[h][:, 1, :], 3, R2, halves[h])
+
+        sums_b0 = bank("y1", [P, 2, P])
+        part = [keep.tile([P, 2, HALF], F32, name=f"part{e}") for e in range(2)]
+        for e in range(2):
+            subtract(e)
+            first_terms(part[e], 2 + e, halves[0])
+            weigh(e)
+            add_turned(sums_b0[:, e, :], [part[e][:, side, :] for side in range(2)])
+            for h in range(2):
+                add_turned(sums_a[1][:, h, e, :], [step[e][:, halves[h]], right[e][:, halves[h]]])
+
+        early = keep.tile([P, 2, P, 2], BF16, name="early")
+        second = [work.tile([P, P, 2], BF16, name="second0", offset=EARLY), keep.tile([P, P, 2], BF16, name="second1")]
+        first = keep.tile([P, P, 2], BF16, name="first")
+        leave(early[:], sums_a[0][:].rearrange("v h e p -> v h p e"))
+        leave(first[:], sums_b0[:].rearrange("v e p -> v p e"))
+        for h in range(2):
+            leave(second[h][:], sums_a[1][:, h].rearrange("v e p -> v p e"))
+
+        def term(dst, t, which, share):
+            nc.vector.tensor_tensor(dst, looked_up(t, which, halves[1]), share, ALU.mult)
+
+        sums_b = [bank("y2", [P, 2, P]), bank("a0", [P, 2, P])]
+        late_a = work.tile([P, HALF], F32, name="late_a", offset=LATE0)
+        late_b = work.tile([P, 3, HALF], F32, name="late_b", offset=EARLY)
+        subtract_b(0, 0)
+        subtract_b(0, 1)
+        subtract_b(1, 0)
+        weigh_b(0)
+        subtract_b(1, 1)
+        term(late_a[:], 2, L1, f[:, 0, halves[1]])
+        weigh_b(1)
+        for h in range(2):
             for e in range(2):
-                parts = [whole[:, i, e, side, :] for side in range(2)]
-                for side in range(2):
-                    gather(parts[side], e, i, side, slice(0, V))
-                for h in range(2):
-                    add_turned(sums[:, h, e, :], [parts[side][:, halves[h]] for side in range(2)])
-            sample = work.tile([P, 2, P, 2], BF16, name=f"early{i}", offset=EARLY + 1024 * i)
-            nc.scalar.activation(sample[:], sums[:].rearrange("v h e p -> v h p e"), ACT.Relu)
-            early.append(sample)
-
-        zb = [bank("y3", [P, 2, HALF]), bank("z", [P, HALF])]
-
-        sums = [bank(f"y{1 + i}", [P, 2, P]) for i in range(2)]
-        first = work.tile([P, 2, P, 2], BF16, name="first", offset=FIRST)
-        n = 0
-        for i in range(2):
-            for e in range(2):
-                parts = []
-                for side in range(2):
-                    part = work.tile([P, HALF], F32, name=f"half{n}", offset=11264 + 512 * n)
-                    gather(part[:], 2 + e, i, side, halves[0])
-                    parts.append(part[:])
-                    n += 1
-                add_turned(sums[i][:, e, :], parts)
-            nc.scalar.activation(first[:, i], sums[i][:].rearrange("v e p -> v p e"), ACT.Relu)
+                add_turned(sums_b[h][:, e, :], [step_b[h][:, e, :], right_b[h][:, e, :]])
+        last_second = keep.tile([P, P, 2], BF16, name="last_second")
+        leave(last_second[:], sums_b[1][:].rearrange("v e p -> v p e"))
 
         z_b = [work.tile([P, HALF, 4], BF16, name="z_b0", align_bytes=64, offset=ZB0), work.tile([P, HALF, 4], BF16, name="z_b1", align_bytes=64, offset=9216)]
         z_words = [z_b[h][:].rearrange("p v t -> p (v t)").bitcast(F32).rearrange("p (v u) -> p v u", u=2) for h in range(2)]
-
         z_c = []
         z_s = [keep.tile([P, HALF], U8, name=f"z_s{h}", align_bytes=64) for h in range(2)]
+        zb = [bank("y3", [P, 2, HALF]), bank("z", [P, HALF])]
 
-        def quantise_z(h):
-            nc.vector.quantize_mx(out=z_c[h][:].bitcast(FP8X4), scales=z_s[h][:], in_=z_b[h][:].rearrange("p v t -> p (v t)"))
-
-        last_sums = bank("s1", [P, 2, P])
-        left0 = keep.tile([P, 2, HALF], F32, name="left0")
-        right0 = keep.tile([P, 2, HALF], F32, name="right0")
-        for e in range(2):
-            gather(left0[:, e, :], 2 + e, 0, 0, halves[1])
-            gather(right0[:, e, :], 2 + e, 0, 1, halves[1])
-            add_turned(last_sums[:, e, :], [left0[:, e, :], right0[:, e, :]])
+        zt0 = keep.tile([P, 2, P, 2], BF16, name="zt0")
         zt1 = keep.tile([P, P, 2], BF16, name="zt1")
-        zt0 = work.tile([P, 2, P, 2], BF16, name="zt0", offset=11264 + 512 * 6)
-        nc.vector.tensor_tensor(zt0[:], early[0][:], early[1][:], ALU.max)
-        nc.vector.tensor_tensor(zt1[:], first[:, 0], first[:, 1], ALU.max)
+        nc.vector.tensor_tensor(zt1[:], sums_b[0][:].rearrange("v e p -> v p e"), first[:], ALU.max)
+        for h in range(2):
+            nc.vector.tensor_tensor(zt0[:, h], early[:, h], second[h][:], ALU.max)
+        term(late_b[:, 0, :], 2, R1, g[:, halves[1]])
+        term(late_b[:, 1, :], 3, L1, f[:, 0, halves[1]])
+        term(late_b[:, 2, :], 3, R1, g[:, halves[1]])
         nc.tensor.transpose(zb[0][:, 0, :], zt0[:, 0].rearrange("v p e -> v (p e)").bitcast(F32), ident[:])
         nc.tensor.transpose(zb[0][:, 1, :], zt1[:].rearrange("v p e -> v (p e)").bitcast(F32), ident[:])
-        last_first = keep.tile([P, P, 2], BF16, name="last_first")
-        nc.scalar.activation(last_first[:], last_sums[:].rearrange("v e p -> v p e"), ACT.Relu)
         nc.scalar.copy(z_words[0], zb[0][:].rearrange("p u v -> p v u"))
-        s1 = bank("a1", [P, HALF])
-        nc.tensor.transpose(s1[:], last_first[:].rearrange("v p e -> v (p e)").bitcast(F32), ident[:])
         nc.tensor.transpose(zb[1][:], zt0[:, 1].rearrange("v p e -> v (p e)").bitcast(F32), ident[:])
         nc.scalar.copy(z_words[1][:, :, 0], zb[1][:])
-        late = [work.tile([P, 2, HALF], F32, name=f"late{e}", offset=(EARLY, FIRST)[e]) for e in range(2)]
-        for e in range(2):
-            for side in range(2):
-                gather(late[e][:, side, :], 2 + e, 1, side, halves[1])
-        s2 = stage.tile([P, 2, HALF], F32, name="s2", offset=HOLD)
-        for e in range(2):
-            nc.vector.tensor_tensor(s2[:, e, :], late[e][:, 0, :], late[e][:, 1, :], ALU.add)
+        back = bank("a1", [P, HALF])
+        nc.tensor.transpose(back[:], last_second[:].rearrange("v p e -> v (p e)").bitcast(F32), ident[:])
+        last_first = keep.tile([P, 2, HALF], F32, name="last_first")
+        nc.vector.tensor_tensor(last_first[:, 0, :], late_a[:], late_b[:, 0, :], ALU.add)
+        nc.vector.tensor_tensor(last_first[:, 1, :], late_b[:, 1, :], late_b[:, 2, :], ALU.add)
         z_c.append(keep.tile([P, HALF], U32, name="z_c0", align_bytes=64))
-        quantise_z(0)
+        nc.vector.quantize_mx(out=z_c[0][:].bitcast(FP8X4), scales=z_s[0][:], in_=z_b[0][:].rearrange("p v t -> p (v t)"))
         quarters = [slice(0, HALF // 2), slice(HALF // 2, HALF)]
         for vs in quarters:
-            nc.vector.tensor_tensor(z_b[1][:, vs, 2:4], s2[:, :, vs].rearrange("p e v -> p v e"), s1[:].bitcast(BF16).rearrange("p (v e) -> p v e", e=2)[:, vs], ALU.max)
+            nc.vector.tensor_tensor(z_b[1][:, vs, 2:4], last_first[:, :, vs].rearrange("p e v -> p v e"), back[:].bitcast(BF16).rearrange("p (v e) -> p v e", e=2)[:, vs], ALU.max)
         z_c.append(work.tile([P, HALF], U32, name="z_c1", align_bytes=64, offset=ZB0))
         for vs in quarters:
             nc.vector.quantize_mx(out=z_c[1][:, vs].bitcast(FP8X4), scales=z_s[1][:, vs], in_=z_b[1][:, vs, :].rearrange("p v t -> p (v t)"))
@@ -223,10 +268,10 @@ def tile_picked_roial_relu_po_kernel(
         nc.sync.dma_start(out_rows[:, :, halves[0]], o_f[:])
         quantise_out(0)
 
-        acc = bank("a0", [P, 4, HALF])
+        acc = bank("s1", [P, 4, HALF])
         for t in range(4):
             product(acc[:, t, :], w2c[:, t, :], w2s[:, t, :], t, z_c[1][:], z_s[1][:])
-        again = bank("a1", [P, 2, HALF])
+        again = bank("y2", [P, 2, HALF])
         for e in range(2):
             product(again[:, e, :], w2c[:, 2 + e, :], w2s[:, 2 + e, :], e, z_c[1][:], z_s[1][:])
         nc.scalar.copy(o_b[1][:], acc[:].rearrange("p t v -> p v t"))

@@ -79,8 +79,9 @@ def tile_picked_roial_relu_po_kernel(
         nc.vector.quantize_mx(out=w1_c[:].bitcast(FP8X4), scales=w1_s[:], in_=w1_b[:].rearrange("p t m j -> p (t m j)"))
 
         x_g = work.tile([P, S], U32, name="x_g", align_bytes=64, offset=7168)
-        for a in range(2):
-            nc.vector.tensor_copy(x_g[:, 256 * a : 256 * (a + 1)], x_win[:].indirect(offs_sb[:, 16 * a : 16 * (a + 1)]))
+        pieces = [slice(0, 256), slice(256, 384), slice(384, S)]
+        for cols in pieces:
+            nc.vector.tensor_copy(x_g[:, cols], x_win[:].indirect(offs_sb[:, cols.start // 16 : cols.stop // 16]))
 
         g = keep.tile([P, V], F32, name="g")
         nc.scalar.activation(g[:], f[:, 0, :], ACT.Copy, bias=1.0, scale=-1.0)
@@ -99,15 +100,14 @@ def tile_picked_roial_relu_po_kernel(
             nc.tensor.matmul_mx(out=dst_ps, lhsT=codes.bitcast(FP8X4), lhsT_scale=scales, rhs=rhs.bitcast(FP8X4), rhs_scale=rhs_scale, start=True, stop=True)
 
         y = [keep.tile([P, S], F32, name=f"y{t}") for t in range(4)]
-        for a in range(2):
-            cols = slice(256 * a, 256 * (a + 1))
-            for t in range(2):
-                acc = bank(("a0", "z", "a1", "y1")[2 * a + t], [P, 256])
-                product(acc[:], w1_c[:, P * t : P * (t + 1)], w1_s[:, P * t : P * (t + 1)], t, x_g[:, cols], xs_g[:, cols])
-                if (a, t) == (0, 1):
-                    nc.vector.tensor_copy(y[t][:, cols], acc[:])
-                else:
-                    nc.scalar.copy(y[t][:, cols], acc[:])
+        passes = [(0, pieces[0], "a0"), (1, pieces[0], "z"), (0, pieces[1], "a1"), (0, pieces[2], "s1"), (1, slice(256, S), "y1")]
+        for t, cols, tag in passes:
+            acc = bank(tag, [P, cols.stop - cols.start])
+            product(acc[:], w1_c[:, P * t : P * (t + 1)], w1_s[:, P * t : P * (t + 1)], t, x_g[:, cols], xs_g[:, cols])
+            if tag == "z":
+                nc.vector.tensor_copy(y[t][:, cols], acc[:])
+            else:
+                nc.scalar.copy(y[t][:, cols], acc[:])
         rest = []
         for t in range(2, 4):
             acc = bank(f"y{t}", [P, S])
@@ -131,6 +131,11 @@ def tile_picked_roial_relu_po_kernel(
         def add_turned(dst_ps, parts):
             for side in range(2):
                 nc.tensor.matmul(dst_ps, parts[side], ident[:], start=(side == 0), stop=(side == 1), is_transpose=True)
+
+        def add_turned_rows(dst_ps, known, late):
+            terms = list(zip(dst_ps, known)) + list(zip(dst_ps, late))
+            for n, (dst, term_sb) in enumerate(terms):
+                nc.tensor.matmul(dst, term_sb, ident[:], start=(n == 0), stop=(n == len(terms) - 1), is_transpose=True)
 
         def leave(dst, sums):
             nc.scalar.activation(dst, sums, ACT.Relu)
@@ -162,8 +167,7 @@ def tile_picked_roial_relu_po_kernel(
         sums_a = [bank(f"s{i}", [P, 2, 2, P]) for i in range(2)]
         for e in range(2):
             first_terms(whole[:, e], e, both)
-            for h in range(2):
-                add_turned(sums_a[0][:, h, e, :], [whole[:, e, side, halves[h]] for side in range(2)])
+            add_turned_rows([sums_a[0][:, h, e, :] for h in range(2)], [whole[:, e, 0, vs] for vs in halves], [whole[:, e, 1, vs] for vs in halves])
 
         fetch(right[0][:], 0, R2, both)
         fetch(left[0][:], 0, L2, both)
@@ -183,8 +187,7 @@ def tile_picked_roial_relu_po_kernel(
             first_terms(part[e], 2 + e, halves[0])
             weigh(e)
             add_turned(sums_b0[:, e, :], [part[e][:, side, :] for side in range(2)])
-            for h in range(2):
-                add_turned(sums_a[1][:, h, e, :], [step[e][:, halves[h]], right[e][:, halves[h]]])
+            add_turned_rows([sums_a[1][:, h, e, :] for h in range(2)], [right[e][:, vs] for vs in halves], [step[e][:, vs] for vs in halves])
 
         early = keep.tile([P, 2, P, 2], BF16, name="early")
         second = [work.tile([P, P, 2], BF16, name="second0", offset=EARLY), keep.tile([P, P, 2], BF16, name="second1")]
@@ -208,8 +211,7 @@ def tile_picked_roial_relu_po_kernel(
         term(late_a[:], 2, L1, f[:, 0, halves[1]])
         weigh_b(1)
         for h in range(2):
-            for e in range(2):
-                add_turned(sums_b[h][:, e, :], [step_b[h][:, e, :], right_b[h][:, e, :]])
+            add_turned_rows([sums_b[h][:, e, :] for e in range(2)], [right_b[h][:, e, :] for e in range(2)], [step_b[h][:, e, :] for e in range(2)])
         last_second = keep.tile([P, P, 2], BF16, name="last_second")
         leave(last_second[:], sums_b[1][:].rearrange("v e p -> v p e"))
 

@@ -192,9 +192,9 @@ def tile_picked_roial_relu_po_kernel(
         early = keep.tile([P, 2, P, 2], BF16, name="early")
         second = [work.tile([P, P, 2], BF16, name="second0", offset=EARLY), keep.tile([P, P, 2], BF16, name="second1")]
         first = keep.tile([P, P, 2], BF16, name="first")
-        leave(early[:], sums_a[0][:].rearrange("v h e p -> v h p e"))
         leave(first[:], sums_b0[:].rearrange("v e p -> v p e"))
         for h in range(2):
+            leave(early[:, h], sums_a[0][:, h].rearrange("v e p -> v p e"))
             leave(second[h][:], sums_a[1][:, h].rearrange("v e p -> v p e"))
 
         def term(dst, t, which, share):
@@ -251,40 +251,23 @@ def tile_picked_roial_relu_po_kernel(
         out_rows = out_0.rearrange("(p t) v -> p t v", t=4)
         out_words = out_1[0].rearrange("p n t -> p (n t)").bitcast(I32)
         o_s = keep.tile([P, V], U8, name="o_s", align_bytes=64)
-        o_c = keep.tile([P, V], I32, name="o_c", align_bytes=64)
-        o_b = [keep.tile([P, HALF, 4], BF16, name=f"o_b{h}", align_bytes=64) for h in range(2)]
-
-        def quantise_out(h):
-            nc.vector.quantize_mx(out=o_c[:, halves[h]].bitcast(FP8X4), scales=o_s[:, halves[h]], in_=o_b[h][:].rearrange("p v t -> p (v t)"))
-
-        acc = bank("s0", [P, 4, HALF])
-        for t in range(4):
-            product(acc[:, t, :], w2c[:, t, :], w2s[:, t, :], t, z_c[0][:], z_s[0][:])
-        again = bank("y1", [P, 2, HALF])
-        for e in range(2):
-            product(again[:, e, :], w2c[:, 2 + e, :], w2s[:, 2 + e, :], e, z_c[0][:], z_s[0][:])
-        nc.scalar.copy(o_b[0][:], acc[:].rearrange("p t v -> p v t"))
-        o_f = work.tile([P, 4, HALF], F32, name="o_f0", offset=9216)
-        nc.vector.tensor_copy(o_f[:, 2:4, :], again[:])
-        nc.scalar.copy(o_f[:, 0:2, :], acc[:, 0:2, :])
-        nc.sync.dma_start(out_rows[:, :, halves[0]], o_f[:])
-        quantise_out(0)
-
-        acc = bank("s1", [P, 4, HALF])
-        for t in range(4):
-            product(acc[:, t, :], w2c[:, t, :], w2s[:, t, :], t, z_c[1][:], z_s[1][:])
-        again = bank("y2", [P, 2, HALF])
-        for e in range(2):
-            product(again[:, e, :], w2c[:, 2 + e, :], w2s[:, 2 + e, :], e, z_c[1][:], z_s[1][:])
-        nc.scalar.copy(o_b[1][:], acc[:].rearrange("p t v -> p v t"))
-        o_hi = keep.tile([P, 2, HALF], F32, name="o_hi")
-        nc.vector.tensor_copy(o_hi[:], again[:])
-        nc.sync.dma_start(out_rows[:, 2:4, halves[1]], o_hi[:])
-        quantise_out(1)
-        nc.sync.dma_start(out_words, o_c[:])
-        o_lo = keep.tile([P, 2, HALF], F32, name="o_lo")
-        nc.scalar.copy(o_lo[:], acc[:, 0:2, :])
-        nc.scalar.dma_start(out_rows[:, 0:2, halves[1]], o_lo[:])
+        for h in range(2):
+            o_f = keep.tile([P, 4, HALF], F32, name=f"o_f{h}")
+            for u in range(2):
+                acc = bank((("s0", "y1"), ("s1", "y2"))[h][u], [P, 2, HALF])
+                for e in range(2):
+                    t = 2 * u + e
+                    product(acc[:, e, :], w2c[:, t, :], w2s[:, t, :], t, z_c[h][:], z_s[h][:])
+                nc.scalar.copy(o_f[:, 2 * u : 2 * u + 2, :], acc[:])
+            nc.sync.dma_start(out_rows[:, :, halves[h]], o_f[:])
+            o_b = work.tile([P, HALF, 4], BF16, name=f"o_b{h}", align_bytes=64, offset=(9216, 10240)[h])
+            o_c = keep.tile([P, HALF], I32, name=f"o_c{h}", align_bytes=64)
+            for vs in quarters:
+                nc.vector.tensor_copy(o_b[:, vs, :], o_f[:, :, vs].rearrange("p t v -> p v t"))
+            for vs in quarters:
+                cols = slice(HALF * h + vs.start, HALF * h + vs.stop)
+                nc.vector.quantize_mx(out=o_c[:, vs].bitcast(FP8X4), scales=o_s[:, cols], in_=o_b[:, vs, :].rearrange("p v t -> p (v t)"))
+            nc.sync.dma_start(out_words[:, halves[h]], o_c[:])
         for q in range(4):
             eng = nc.sync if q < 2 else nc.scalar
             eng.dma_start(out_2[0][4 * q : 4 * q + 4, :].bitcast(I32), o_s[32 * q : 32 * q + 4, :].bitcast(I32))

@@ -140,7 +140,7 @@ def tile_picked_roial_relu_po_kernel(
         def leave(dst, sums):
             nc.scalar.activation(dst, sums, ACT.Relu)
 
-        EARLY, LATE0, ZB0 = 0, 3072, 5632
+        EARLY, LATE0, LATE1, ZB0 = 0, 3072, 4096, 5632
         left = [keep.tile([P, V], F32, name=f"left{t}") for t in range(2)]
         right = [keep.tile([P, V], F32, name=f"right{t}") for t in range(2)]
         step = [keep.tile([P, V], F32, name=f"step{t}") for t in range(2)]
@@ -148,7 +148,7 @@ def tile_picked_roial_relu_po_kernel(
         left_b = [keep.tile([P, HALF], F32, name="left_b0"), work.tile([P, HALF], F32, name="left_b1", offset=LATE0)]
         right_b = [keep.tile([P, 2, HALF], F32, name=f"right_b{h}") for h in range(2)]
         step_b = [keep.tile([P, 2, HALF], F32, name=f"step_b{h}") for h in range(2)]
-        diff_b = [keep.tile([P, 2, HALF], F32, name=f"diff_b{h}") for h in range(2)]
+        diff_b = [keep.tile([P, 2, HALF], F32, name="diff_b0"), work.tile([P, 2, HALF], F32, name="diff_b1", offset=LATE1)]
 
         def subtract(t):
             nc.vector.tensor_tensor(diff[t][:], left[t][:], right[t][:], ALU.subtract)
@@ -202,7 +202,7 @@ def tile_picked_roial_relu_po_kernel(
 
         sums_b = [bank("y2", [P, 2, P]), bank("a0", [P, 2, P])]
         late_a = work.tile([P, HALF], F32, name="late_a", offset=LATE0)
-        late_b = work.tile([P, 3, HALF], F32, name="late_b", offset=EARLY)
+        late_b = work.tile([P, HALF], F32, name="late_b", offset=EARLY)
         subtract_b(0, 0)
         subtract_b(0, 1)
         subtract_b(1, 0)
@@ -212,6 +212,9 @@ def tile_picked_roial_relu_po_kernel(
         weigh_b(1)
         for h in range(2):
             add_turned_rows([sums_b[h][:, e, :] for e in range(2)], [right_b[h][:, e, :] for e in range(2)], [step_b[h][:, e, :] for e in range(2)])
+        late_r = work.tile([P, 2, HALF], F32, name="late_r", offset=LATE1)
+        for e in range(2):
+            fetch(late_r[:, e, :], 2 + e, R1, halves[1])
         last_second = keep.tile([P, P, 2], BF16, name="last_second")
         leave(last_second[:], sums_b[1][:].rearrange("v e p -> v p e"))
 
@@ -226,9 +229,10 @@ def tile_picked_roial_relu_po_kernel(
         nc.vector.tensor_tensor(zt1[:], sums_b[0][:].rearrange("v e p -> v p e"), first[:], ALU.max)
         for h in range(2):
             nc.vector.tensor_tensor(zt0[:, h], early[:, h], second[h][:], ALU.max)
-        term(late_b[:, 0, :], 2, R1, g[:, halves[1]])
-        term(late_b[:, 1, :], 3, L1, f[:, 0, halves[1]])
-        term(late_b[:, 2, :], 3, R1, g[:, halves[1]])
+        term(late_b[:], 3, L1, f[:, 0, halves[1]])
+        late_m = keep.tile([P, 2, HALF], F32, name="late_m")
+        for e in range(2):
+            nc.vector.tensor_tensor(late_m[:, e, :], late_r[:, e, :], g[:, halves[1]], ALU.mult)
         nc.tensor.transpose(zb[0][:, 0, :], zt0[:, 0].rearrange("v p e -> v (p e)").bitcast(F32), ident[:])
         nc.tensor.transpose(zb[0][:, 1, :], zt1[:].rearrange("v p e -> v (p e)").bitcast(F32), ident[:])
         nc.scalar.copy(z_words[0], zb[0][:].rearrange("p u v -> p v u"))
@@ -237,8 +241,8 @@ def tile_picked_roial_relu_po_kernel(
         back = bank("a1", [P, HALF])
         nc.tensor.transpose(back[:], last_second[:].rearrange("v p e -> v (p e)").bitcast(F32), ident[:])
         last_first = keep.tile([P, 2, HALF], F32, name="last_first")
-        nc.vector.tensor_tensor(last_first[:, 0, :], late_a[:], late_b[:, 0, :], ALU.add)
-        nc.vector.tensor_tensor(last_first[:, 1, :], late_b[:, 1, :], late_b[:, 2, :], ALU.add)
+        nc.vector.tensor_tensor(last_first[:, 0, :], late_a[:], late_m[:, 0, :], ALU.add)
+        nc.vector.tensor_tensor(last_first[:, 1, :], late_b[:], late_m[:, 1, :], ALU.add)
         z_c.append(keep.tile([P, HALF], U32, name="z_c0", align_bytes=64))
         nc.vector.quantize_mx(out=z_c[0][:].bitcast(FP8X4), scales=z_s[0][:], in_=z_b[0][:].rearrange("p v t -> p (v t)"))
         quarters = [slice(0, HALF // 2), slice(HALF // 2, HALF)]

@@ -79,7 +79,7 @@ def tile_picked_roial_relu_po_kernel(
         nc.vector.quantize_mx(out=w1_c[:].bitcast(FP8X4), scales=w1_s[:], in_=w1_b[:].rearrange("p t m j -> p (t m j)"))
 
         x_g = work.tile([P, S], U32, name="x_g", align_bytes=64, offset=7168)
-        pieces = [slice(0, 256), slice(256, 384), slice(384, S)]
+        pieces = [slice(P * n, P * (n + 1)) for n in range(4)]
         for cols in pieces:
             nc.vector.tensor_copy(x_g[:, cols], x_win[:].indirect(offs_sb[:, cols.start // 16 : cols.stop // 16]))
 
@@ -100,19 +100,26 @@ def tile_picked_roial_relu_po_kernel(
             nc.tensor.matmul_mx(out=dst_ps, lhsT=codes.bitcast(FP8X4), lhsT_scale=scales, rhs=rhs.bitcast(FP8X4), rhs_scale=rhs_scale, start=True, stop=True)
 
         y = [keep.tile([P, S], F32, name=f"y{t}") for t in range(4)]
-        passes = [(0, pieces[0], "a0"), (1, pieces[0], "z"), (0, pieces[1], "a1"), (0, pieces[2], "s1"), (1, slice(256, S), "y1")]
-        for t, cols, tag in passes:
-            acc = bank(tag, [P, cols.stop - cols.start])
-            product(acc[:], w1_c[:, P * t : P * (t + 1)], w1_s[:, P * t : P * (t + 1)], t, x_g[:, cols], xs_g[:, cols])
-            if tag == "z":
-                nc.vector.tensor_copy(y[t][:, cols], acc[:])
-            else:
-                nc.scalar.copy(y[t][:, cols], acc[:])
-        rest = []
+        def project(dst_ps, t, cols):
+            product(dst_ps, w1_c[:, P * t : P * (t + 1)], w1_s[:, P * t : P * (t + 1)], t, x_g[:, cols], xs_g[:, cols])
+
+        y0_ps = [bank(tag, [P, P]) for tag in ("a0", "a1", "s1", "s0")]
+        y1_ps = [bank(tag, [P, 256]) for tag in ("z", "y1")]
+        rest = [bank(f"y{t}", [P, S]) for t in range(2, 4)]
+        project(y0_ps[0][:], 0, pieces[0])
+        nc.scalar.copy(y[0][:, pieces[0]], y0_ps[0][:])
+        project(y1_ps[0][:, pieces[0]], 1, pieces[0])
+        project(y0_ps[1][:], 0, pieces[1])
+        nc.scalar.copy(y[0][:, pieces[1]], y0_ps[1][:])
+        project(y1_ps[0][:, pieces[1]], 1, pieces[1])
+        nc.vector.tensor_copy(y[1][:, 0:256], y1_ps[0][:])
+        for n in range(2, 4):
+            project(y0_ps[n][:], 0, pieces[n])
+            nc.scalar.copy(y[0][:, pieces[n]], y0_ps[n][:])
+        project(y1_ps[1][:], 1, slice(256, S))
+        nc.scalar.copy(y[1][:, 256:S], y1_ps[1][:])
         for t in range(2, 4):
-            acc = bank(f"y{t}", [P, S])
-            product(acc[:], w1_c[:, P * t : P * (t + 1)], w1_s[:, P * t : P * (t + 1)], t, x_g[:], xs_g[:])
-            rest.append(acc)
+            project(rest[t - 2][:], t, slice(0, S))
 
         halves = [slice(0, HALF), slice(HALF, V)]
         both = slice(0, V)

@@ -91,7 +91,7 @@ def tile_picked_roial_relu_po_kernel(
         for q in range(4):
             nc.sync.dma_start(w2s[32 * q : 32 * q + 4].rearrange("p t m -> p (t m)").bitcast(I32), w2s_rows[ROWS + 4 * q : ROWS + 4 * q + 4].rearrange("p t m -> p (t m)").bitcast(I32))
         w2c = stage.tile([P, 4, P], I32, name="w2c", align_bytes=64, offset=X + 6144)
-        nc.vector.tensor_copy(w2c[:].rearrange("p t m -> p m t"), w2_raw[:].rearrange("p (m t) -> p m t", t=4))
+        nc.vector.tensor_copy(w2c[:].rearrange("p t (c i) -> p c t i", i=4), w2_raw[:].rearrange("p (c i t) -> p c t i", i=4, t=4))
 
         def bank(tag, shape):
             return psum.tile(shape, F32, name=tag, tag=tag)
@@ -274,7 +274,7 @@ def tile_picked_roial_relu_po_kernel(
             o_b = work.tile([P, HALF, 4], BF16, name=f"o_b{h}", align_bytes=64, offset=(9216, 10240)[h])
             o_c = keep.tile([P, HALF], I32, name=f"o_c{h}", align_bytes=64)
             for vs in quarters:
-                nc.vector.tensor_copy(o_b[:, vs, :], o_f[:, :, vs].rearrange("p t v -> p v t"))
+                nc.vector.tensor_copy(o_b[:, vs, :].rearrange("p (c i) t -> p c t i", i=4), o_f[:, :, vs].rearrange("p t (c i) -> p c t i", i=4))
             for vs in quarters:
                 cols = slice(HALF * h + vs.start, HALF * h + vs.stop)
                 nc.vector.quantize_mx(out=o_c[:, vs].bitcast(FP8X4), scales=o_s[:, cols], in_=o_b[:, vs, :].rearrange("p v t -> p (v t)"))

@@ -269,8 +269,9 @@ def tile_picked_roial_relu_po_kernel(
                 for e in range(2):
                     t = 2 * u + e
                     product(acc[:, e, :], w2c[:, t, :], w2s[:, t, :], t, z_c[h][:], z_s[h][:])
-                nc.scalar.copy(o_f[:, 2 * u : 2 * u + 2, :], acc[:])
-            nc.sync.dma_start(out_rows[:, :, halves[h]], o_f[:])
+                for vs in [slice(0, HALF)] if u == 0 else quarters:
+                    nc.scalar.copy(o_f[:, 2 * u : 2 * u + 2, vs], acc[:, :, vs])
+                nc.sync.dma_start(out_rows[:, 2 * u : 2 * u + 2, halves[h]], o_f[:, 2 * u : 2 * u + 2, :])
             o_b = work.tile([P, HALF, 4], BF16, name=f"o_b{h}", align_bytes=64, offset=(9216, 10240)[h])
             o_c = keep.tile([P, HALF], I32, name=f"o_c{h}", align_bytes=64)
             for vs in quarters:

@@ -199,10 +199,10 @@ def tile_picked_roial_relu_po_kernel(
         early = keep.tile([P, 2, P, 2], BF16, name="early")
         second = [work.tile([P, P, 2], BF16, name="second0", offset=EARLY), keep.tile([P, P, 2], BF16, name="second1")]
         first = keep.tile([P, P, 2], BF16, name="first")
-        leave(first[:], sums_b0[:].rearrange("v e p -> v p e"))
+        nc.scalar.copy(first[:], sums_b0[:].rearrange("v e p -> v p e"))
         for h in range(2):
             leave(early[:, h], sums_a[0][:, h].rearrange("v e p -> v p e"))
-            leave(second[h][:], sums_a[1][:, h].rearrange("v e p -> v p e"))
+            nc.scalar.copy(second[h][:], sums_a[1][:, h].rearrange("v e p -> v p e"))
 
         def term(dst, t, which, share):
             nc.vector.tensor_tensor(dst, looked_up(t, which, halves[1]), share, ALU.mult)
@@ -223,7 +223,7 @@ def tile_picked_roial_relu_po_kernel(
         for e in range(2):
             fetch(late_r[:, e, :], 2 + e, R1, halves[1])
         last_second = keep.tile([P, P, 2], BF16, name="last_second")
-        leave(last_second[:], sums_b[1][:].rearrange("v e p -> v p e"))
+        nc.scalar.copy(last_second[:], sums_b[1][:].rearrange("v e p -> v p e"))
 
         z_b = [work.tile([P, HALF, 4], BF16, name="z_b0", align_bytes=64, offset=ZB0), work.tile([P, HALF, 4], BF16, name="z_b1", align_bytes=64, offset=9216)]
         z_words = [z_b[h][:].rearrange("p v t -> p (v t)").bitcast(F32).rearrange("p (v u) -> p v u", u=2) for h in range(2)]
@@ -233,7 +233,7 @@ def tile_picked_roial_relu_po_kernel(
 
         zt0 = keep.tile([P, 2, P, 2], BF16, name="zt0")
         zt1 = keep.tile([P, P, 2], BF16, name="zt1")
-        nc.vector.tensor_tensor(zt1[:], sums_b[0][:].rearrange("v e p -> v p e"), first[:], ALU.max)
+        nc.vector.scalar_tensor_tensor(zt1[:], sums_b[0][:].rearrange("v e p -> v p e"), 0.0, first[:], ALU.max, ALU.max)
         for h in range(2):
             nc.vector.tensor_tensor(zt0[:, h], early[:, h], second[h][:], ALU.max)
         term(late_b[:], 3, L1, f[:, 0, halves[1]])
@@ -254,7 +254,7 @@ def tile_picked_roial_relu_po_kernel(
         nc.vector.quantize_mx(out=z_c[0][:].bitcast(FP8X4), scales=z_s[0][:], in_=z_b[0][:].rearrange("p v t -> p (v t)"))
         quarters = [slice(0, HALF // 2), slice(HALF // 2, HALF)]
         for vs in quarters:
-            nc.vector.tensor_tensor(z_b[1][:, vs, 2:4], last_first[:, :, vs].rearrange("p e v -> p v e"), back[:].bitcast(BF16).rearrange("p (v e) -> p v e", e=2)[:, vs], ALU.max)
+            nc.vector.scalar_tensor_tensor(z_b[1][:, vs, 2:4], last_first[:, :, vs].rearrange("p e v -> p v e"), 0.0, back[:].bitcast(BF16).rearrange("p (v e) -> p v e", e=2)[:, vs], ALU.max, ALU.max)
         z_c.append(work.tile([P, HALF], U32, name="z_c1", align_bytes=64, offset=ZB0))
         for vs in quarters:
             nc.vector.quantize_mx(out=z_c[1][:, vs].bitcast(FP8X4), scales=z_s[1][:, vs], in_=z_b[1][:, vs, :].rearrange("p v t -> p (v t)"))

@@ -43,8 +43,8 @@ def tile_picked_roial_relu_po_kernel(
 
         nc.scalar.dma_start(xs_win[ROWS:, :].bitcast(I32), x_scales[0].bitcast(I32))
         nc.sync.dma_start(offs_sb[:], offs)
-        nc.scalar.dma_start(w2s_raw[ROWS:, :].bitcast(I32), w2_scales[0].bitcast(I32))
         nc.sync.dma_start(w1_raw[:], w1.rearrange("(p j) c -> p j c", j=4))
+        nc.sync.dma_start(w2s_raw[ROWS:, :].bitcast(I32), w2_scales[0].bitcast(I32))
         nc.sync.dma_start(lists[0][:], l1)
         nc.sync.dma_start(lists[1][:], r1)
         nc.sync.dma_start(lists[2][:], l2)

from contextlib import ExitStack

import concourse.mybir as mybir
from concourse.masks import make_identity

K, T, S, V, N, H = 512, 2048, 512, 256, 512, 512
FLOPS = 2 * K * H * S + 2 * H * N * V
BYTES = K * T + K * T // 32 + 4 * K * H + 2 * 8 * V * 4 + H * N + H * N // 32 + 2 * 128 * (32 + 4 * 16) + 4 * N * V + N * V + N * V // 32

F32 = mybir.dt.float32
BF16 = mybir.dt.bfloat16
I32 = mybir.dt.int32
U32 = mybir.dt.uint32
U16 = mybir.dt.uint16
U8 = mybir.dt.uint8
FP8X4 = mybir.dt.float8_e4m3fn_x4
ALU = mybir.AluOpType
ACT = mybir.ActivationFunctionType

P = 128
HALF = 128
SPLIT = 88


def tile_picked_roial_relu_po_kernel(
    tc, x_words, x_scales, w1, fr1, fr2, w2_words, w2_scales, offs, l1, r1, l2, r2, out_0, out_1, out_2
):
    nc = tc.nc
    with ExitStack() as ctx:
        keep = ctx.enter_context(tc.tile_pool(name="keep", bufs=1))
        stage = ctx.enter_context(tc.tile_pool(name="stage", bufs=1))
        work = ctx.enter_context(tc.tile_pool(name="work", bufs=1))
        psum = ctx.enter_context(tc.psum_pool(name="psum", bufs=1))

        offs_sb = keep.tile([P, S // 16], U16, name="offs_sb")
        lists = [keep.tile([P, V // 16], U16, name=f"list{i}") for i in range(4)]
        W1, X, XS, W1B, HOLD, ROWS = 0, 8192, 16384, 18432, 22528, 112
        w1_raw = stage.tile([P, 4, H], F32, name="w1_raw", offset=W1)
        x_win = stage.tile([P, T], U32, name="x_win", offset=X)
        xs_win = stage.tile([P, T], U8, name="xs_win", offset=XS)
        ident = keep.tile([P, P], F32, name="ident")
        w2s_raw = stage.tile([P, N], U8, name="w2s_raw", offset=HOLD + 2048 - 256)

        nc.scalar.dma_start(xs_win[ROWS:, :].bitcast(I32), x_scales[0].bitcast(I32))
        nc.sync.dma_start(offs_sb[:], offs)
        nc.sync.dma_start(w1_raw[:], w1.rearrange("(p j) c -> p j c", j=4))
        nc.sync.dma_start(w2s_raw[ROWS:, :].bitcast(I32), w2_scales[0].bitcast(I32))
        nc.sync.dma_start(lists[0][:], l1)
        nc.sync.dma_start(lists[1][:], r1)
        nc.sync.dma_start(lists[2][:], l2)
        nc.sync.dma_start(x_win[:].bitcast(I32), x_words[0].rearrange("p n t -> p (n t)").bitcast(I32))
        nc.sync.dma_start(lists[3][:], r2)
        nc.vector.memset(xs_win[:ROWS, :].bitcast(I32), 0)
        xs_g = keep.tile([P, S], U8, name="xs_g", align_bytes=64)
        nc.vector.memset(xs_g[:].bitcast(I32), 0)
        nc.vector.memset(w2s_raw[:ROWS, :].bitcast(I32), 0)
        make_identity(nc, ident[:])

        xs_rows = keep.tile([P, S], U8, name="xs_rows")
        nc.vector.tensor_copy(xs_rows[:], xs_win[:].indirect(offs_sb[:]))
        for q in range(4):
            nc.sync.dma_start(xs_g[32 * q : 32 * q + 4, :].bitcast(I32), xs_rows[ROWS + 4 * q : ROWS + 4 * q + 4, :].bitcast(I32))

        w2s_rows = stage.tile([P, 4, P], U8, name="w2s_rows", offset=XS)
        nc.vector.tensor_copy(w2s_rows[:], w2s_raw[:].rearrange("p (m t) -> p t m", t=4))

        w1_b = stage.tile([P, 4, P, 4], BF16, name="w1_b", align_bytes=64, offset=W1B)
        src = w1_raw[:].rearrange("p j (m t) -> p m j t", t=4)
        dst = w1_b[:].rearrange("p t m j -> p m j t")
        nc.vector.tensor_copy(dst[:, :SPLIT], src[:, :SPLIT])
        nc.scalar.copy(dst[:, SPLIT:], src[:, SPLIT:])
        f = stage.tile([P, 2, V], F32, name="f", offset=HOLD)
        w2_raw = stage.tile([P, N], I32, name="w2_raw", offset=HOLD + 2048)
        nc.sync.dma_start(f[:, 0, :], fr1.rearrange("(p t) v -> p t v", t=4)[:, 0, :])
        nc.sync.dma_start(w2_raw[:], w2_words[0].rearrange("p n t -> p (n t)").bitcast(I32))
        nc.sync.dma_start(f[:, 1, :], fr2.rearrange("(p t) v -> p t v", t=4)[:, 0, :])
        w1_c = keep.tile([P, H], U32, name="w1_c", align_bytes=64)
        w1_s = keep.tile([P, H], U8, name="w1_s", align_bytes=64)
        nc.vector.quantize_mx(out=w1_c[:].bitcast(FP8X4), scales=w1_s[:], in_=w1_b[:].rearrange("p t m j -> p (t m j)"))

        x_g = work.tile([P, S], U32, name="x_g", align_bytes=64, offset=7168)
        pieces = [slice(P * n, P * (n + 1)) for n in range(4)]
        for cols in pieces:
            nc.vector.tensor_copy(x_g[:, cols], x_win[:].indirect(offs_sb[:, cols.start // 16 : cols.stop // 16]))

        g = keep.tile([P, V], F32, name="g")
        nc.scalar.activation(g[:], f[:, 0, :], ACT.Copy, bias=1.0, scale=-1.0)

        w2s = stage.tile([P, 4, P], U8, name="w2s", align_bytes=64, offset=W1B)
        nc.vector.memset(w2s[:].rearrange("p t m -> p (t m)").bitcast(I32), 0)
        for q in range(4):
            nc.sync.dma_start(w2s[32 * q : 32 * q + 4].rearrange("p t m -> p (t m)").bitcast(I32), w2s_rows[ROWS + 4 * q : ROWS + 4 * q + 4].rearrange("p t m -> p (t m)").bitcast(I32))
        w2c = stage.tile([P, 4, P], I32, name="w2c", align_bytes=64, offset=X + 6144)
        nc.vector.tensor_copy(w2c[:].rearrange("p t (c i) -> p c t i", i=4), w2_raw[:].rearrange("p (c i t) -> p c t i", i=4, t=4))

        def bank(tag, shape):
            return psum.tile(shape, F32, name=tag, tag=tag)

        def product(dst_ps, codes, scales, t, rhs, rhs_scale):
            nc.tensor.matmul_mx(out=dst_ps, lhsT=codes.bitcast(FP8X4), lhsT_scale=scales, rhs=rhs.bitcast(FP8X4), rhs_scale=rhs_scale, start=True, stop=True)

        y = [keep.tile([P, S], F32, name=f"y{t}") for t in range(4)]
        def project(dst_ps, t, cols):
            product(dst_ps, w1_c[:, P * t : P * (t + 1)], w1_s[:, P * t : P * (t + 1)], t, x_g[:, cols], xs_g[:, cols])

        y0_ps = [bank(tag, [P, P]) for tag in ("a0", "a1", "s1", "s0")]
        y1_ps = [bank(tag, [P, 256]) for tag in ("z", "y1")]
        rest = [bank(f"y{t}", [P, S]) for t in range(2, 4)]
        project(y0_ps[0][:], 0, pieces[0])
        nc.scalar.copy(y[0][:, pieces[0]], y0_ps[0][:])
        project(y1_ps[0][:, pieces[0]], 1, pieces[0])
        project(y0_ps[1][:], 0, pieces[1])
        nc.scalar.copy(y[0][:, pieces[1]], y0_ps[1][:])
        project(y1_ps[0][:, pieces[1]], 1, pieces[1])
        nc.vector.tensor_copy(y[1][:, 0:256], y1_ps[0][:])
        for n in range(2, 4):
            project(y0_ps[n][:], 0, pieces[n])
            nc.scalar.copy(y[0][:, pieces[n]], y0_ps[n][:])
        project(y1_ps[1][:], 1, slice(256, S))
        nc.scalar.copy(y[1][:, 256:S], y1_ps[1][:])
        for t in range(2, 4):
            project(rest[t - 2][:], t, slice(0, S))

        halves = [slice(0, HALF), slice(HALF, V)]
        both = slice(0, V)
        L1, R1, L2, R2 = range(4)

        def looked_up(t, which, vs):
            return y[t][:].indirect(lists[which][:, vs.start // 16 : vs.stop // 16])

        def first_terms(dst, t, vs):
            nc.vector.tensor_tensor(dst[:, 0, :], looked_up(t, L1, vs), f[:, 0, vs], ALU.mult)
            nc.vector.tensor_tensor(dst[:, 1, :], looked_up(t, R1, vs), g[:, vs], ALU.mult)

        def fetch(dst, t, which, vs):
            nc.scalar.activation(dst, looked_up(t, which, vs), ACT.Copy)

        def add_turned(dst_ps, parts):
            for side in range(2):
                nc.tensor.matmul(dst_ps, parts[side], ident[:], start=(side == 0), stop=(side == 1), is_transpose=True)

        def add_turned_rows(dst_ps, known, late):
            terms = list(zip(dst_ps, known)) + list(zip(dst_ps, late))
            for n, (dst, term_sb) in enumerate(terms):
                nc.tensor.matmul(dst, term_sb, ident[:], start=(n == 0), stop=(n == len(terms) - 1), is_transpose=True)

        def leave(dst, sums):
            nc.scalar.activation(dst, sums, ACT.Relu)

        EARLY, LATE0, LATE1, ZB0 = 0, 3072, 4096, 5632
        left = [keep.tile([P, V], F32, name=f"left{t}") for t in range(2)]
        right = [keep.tile([P, V], F32, name=f"right{t}") for t in range(2)]
        step = [keep.tile([P, V], F32, name=f"step{t}") for t in range(2)]
        diff = [keep.tile([P, V], F32, name=f"diff{t}") for t in range(2)]
        left_b = [keep.tile([P, HALF], F32, name="left_b0"), work.tile([P, HALF], F32, name="left_b1", offset=LATE0)]
        right_b = [keep.tile([P, 2, HALF], F32, name=f"right_b{h}") for h in range(2)]
        step_b = [keep.tile([P, 2, HALF], F32, name=f"step_b{h}") for h in range(2)]
        diff_b = [keep.tile([P, 2, HALF], F32, name="diff_b0"), work.tile([P, 2, HALF], F32, name="diff_b1", offset=LATE1)]

        def subtract(t):
            nc.vector.tensor_tensor(diff[t][:], left[t][:], right[t][:], ALU.subtract)

        def weigh(t):
            nc.vector.tensor_tensor(step[t][:], diff[t][:], f[:, 1, :], ALU.mult)

        def subtract_b(h, e):
            lhs = left_b[h][:] if e == 0 else looked_up(3, L2, halves[h])
            nc.vector.tensor_tensor(diff_b[h][:, e, :], lhs, right_b[h][:, e, :], ALU.subtract)

        def weigh_b(h):
            nc.vector.tensor_tensor(step_b[h][:], diff_b[h][:], f[:, 1:2, halves[h]].to_broadcast([P, 2, HALF]), ALU.mult)

        whole = stage.tile([P, 2, 2, V], F32, name="whole", offset=HOLD + 2048)
        sums_a = [bank(f"s{i}", [P, 2, 2, P]) for i in range(2)]
        for e in range(2):
            first_terms(whole[:, e], e, both)
            add_turned_rows([sums_a[0][:, h, e, :] for h in range(2)], [whole[:, e, 0, vs] for vs in halves], [whole[:, e, 1, vs] for vs in halves])

        fetch(right[0][:], 0, R2, both)
        fetch(left[0][:], 0, L2, both)
        for t in range(2, 4):
            nc.scalar.copy(y[t][:], rest[t - 2][:])
        fetch(right[1][:], 1, R2, both)
        fetch(left[1][:], 1, L2, both)
        for h in range(2):
            fetch(right_b[h][:, 0, :], 2, R2, halves[h])
            fetch(left_b[h][:], 2, L2, halves[h])
            fetch(right_b[h][:, 1, :], 3, R2, halves[h])

        sums_b0 = bank("y1", [P, 2, P])
        part = [keep.tile([P, 2, HALF], F32, name=f"part{e}") for e in range(2)]
        for e in range(2):
            subtract(e)
            first_terms(part[e], 2 + e, halves[0])
            weigh(e)
            add_turned(sums_b0[:, e, :], [part[e][:, side, :] for side in range(2)])
            add_turned_rows([sums_a[1][:, h, e, :] for h in range(2)], [right[e][:, vs] for vs in halves], [step[e][:, vs] for vs in halves])

        early = keep.tile([P, 2, P, 2], BF16, name="early")
        second = [work.tile([P, P, 2], BF16, name="second0", offset=EARLY), keep.tile([P, P, 2], BF16, name="second1")]
        first = keep.tile([P, P, 2], BF16, name="first")
        nc.scalar.copy(first[:], sums_b0[:].rearrange("v e p -> v p e"))
        for h in range(2):
            leave(early[:, h], sums_a[0][:, h].rearrange("v e p -> v p e"))
            nc.scalar.copy(second[h][:], sums_a[1][:, h].rearrange("v e p -> v p e"))

        def term(dst, t, which, share):
            nc.vector.tensor_tensor(dst, looked_up(t, which, halves[1]), share, ALU.mult)

        sums_b = [bank("y2", [P, 2, P]), bank("a0", [P, 2, P])]
        late_a = work.tile([P, HALF], F32, name="late_a", offset=LATE0)
        late_b = work.tile([P, HALF], F32, name="late_b", offset=EARLY)
        subtract_b(0, 0)
        subtract_b(0, 1)
        subtract_b(1, 0)
        weigh_b(0)
        subtract_b(1, 1)
        term(late_a[:], 2, L1, f[:, 0, halves[1]])
        weigh_b(1)
        for h in range(2):
            add_turned_rows([sums_b[h][:, e, :] for e in range(2)], [right_b[h][:, e, :] for e in range(2)], [step_b[h][:, e, :] for e in range(2)])
        late_r = work.tile([P, 2, HALF], F32, name="late_r", offset=LATE1)
        for e in range(2):
            fetch(late_r[:, e, :], 2 + e, R1, halves[1])
        last_second = keep.tile([P, P, 2], BF16, name="last_second")
        nc.scalar.copy(last_second[:], sums_b[1][:].rearrange("v e p -> v p e"))

        z_b = [work.tile([P, HALF, 4], BF16, name="z_b0", align_bytes=64, offset=ZB0), work.tile([P, HALF, 4], BF16, name="z_b1", align_bytes=64, offset=9216)]
        z_words = [z_b[h][:].rearrange("p v t -> p (v t)").bitcast(F32).rearrange("p (v u) -> p v u", u=2) for h in range(2)]
        z_c = []
        z_s = [keep.tile([P, HALF], U8, name=f"z_s{h}", align_bytes=64) for h in range(2)]
        zb = [bank("y3", [P, 2, HALF]), bank("z", [P, HALF])]

        zt0 = keep.tile([P, 2, P, 2], BF16, name="zt0")
        zt1 = keep.tile([P, P, 2], BF16, name="zt1")
        nc.vector.scalar_tensor_tensor(zt1[:], sums_b[0][:].rearrange("v e p -> v p e"), 0.0, first[:], ALU.max, ALU.max)
        for h in range(2):
            nc.vector.tensor_tensor(zt0[:, h], early[:, h], second[h][:], ALU.max)
        term(late_b[:], 3, L1, f[:, 0, halves[1]])
        late_m = keep.tile([P, 2, HALF], F32, name="late_m")
        for e in range(2):
            nc.vector.tensor_tensor(late_m[:, e, :], late_r[:, e, :], g[:, halves[1]], ALU.mult)
        nc.tensor.transpose(zb[0][:, 0, :], zt0[:, 0].rearrange("v p e -> v (p e)").bitcast(F32), ident[:])
        nc.tensor.transpose(zb[0][:, 1, :], zt1[:].rearrange("v p e -> v (p e)").bitcast(F32), ident[:])
        nc.scalar.copy(z_words[0], zb[0][:].rearrange("p u v -> p v u"))
        nc.tensor.transpose(zb[1][:], zt0[:, 1].rearrange("v p e -> v (p e)").bitcast(F32), ident[:])
        nc.scalar.copy(z_words[1][:, :, 0], zb[1][:])
        back = bank("a1", [P, HALF])
        nc.tensor.transpose(back[:], last_second[:].rearrange("v p e -> v (p e)").bitcast(F32), ident[:])
        last_first = keep.tile([P, 2, HALF], F32, name="last_first")
        nc.vector.tensor_tensor(last_first[:, 0, :], late_a[:], late_m[:, 0, :], ALU.add)
        nc.vector.tensor_tensor(last_first[:, 1, :], late_b[:], late_m[:, 1, :], ALU.add)
        z_c.append(keep.tile([P, HALF], U32, name="z_c0", align_bytes=64))
        nc.vector.quantize_mx(out=z_c[0][:].bitcast(FP8X4), scales=z_s[0][:], in_=z_b[0][:].rearrange("p v t -> p (v t)"))
        quarters = [slice(0, HALF // 2), slice(HALF // 2, HALF)]
        for vs in quarters:
            nc.vector.scalar_tensor_tensor(z_b[1][:, vs, 2:4], last_first[:, :, vs].rearrange("p e v -> p v e"), 0.0, back[:].bitcast(BF16).rearrange("p (v e) -> p v e", e=2)[:, vs], ALU.max, ALU.max)
        z_c.append(work.tile([P, HALF], U32, name="z_c1", align_bytes=64, offset=ZB0))
        for vs in quarters:
            nc.vector.quantize_mx(out=z_c[1][:, vs].bitcast(FP8X4), scales=z_s[1][:, vs], in_=z_b[1][:, vs, :].rearrange("p v t -> p (v t)"))

        out_rows = out_0.rearrange("(p t) v -> p t v", t=4)
        out_words = out_1[0].rearrange("p n t -> p (n t)").bitcast(I32)
        o_s = keep.tile([P, V], U8, name="o_s", align_bytes=64)
        for h in range(2):
            o_f = keep.tile([P, 4, HALF], F32, name=f"o_f{h}")
            for u in range(2):
                acc = bank((("s0", "y1"), ("s1", "y2"))[h][u], [P, 2, HALF])
                for e in range(2):
                    t = 2 * u + e
                    product(acc[:, e, :], w2c[:, t, :], w2s[:, t, :], t, z_c[h][:], z_s[h][:])
                for vs in [slice(0, HALF)] if u == 0 else quarters:
                    nc.scalar.copy(o_f[:, 2 * u : 2 * u + 2, vs], acc[:, :, vs])
                nc.sync.dma_start(out_rows[:, 2 * u : 2 * u + 2, halves[h]], o_f[:, 2 * u : 2 * u + 2, :])
            o_b = work.tile([P, HALF, 4], BF16, name=f"o_b{h}", align_bytes=64, offset=(9216, 10240)[h])
            o_c = keep.tile([P, HALF], I32, name=f"o_c{h}", align_bytes=64)
            for vs in quarters:
                nc.vector.tensor_copy(o_b[:, vs, :].rearrange("p (c i) t -> p c t i", i=4), o_f[:, :, vs].rearrange("p t (c i) -> p c t i", i=4))
            for vs in quarters:
                cols = slice(HALF * h + vs.start, HALF * h + vs.stop)
                nc.vector.quantize_mx(out=o_c[:, vs].bitcast(FP8X4), scales=o_s[:, cols], in_=o_b[:, vs, :].rearrange("p v t -> p (v t)"))
            nc.sync.dma_start(out_words[:, halves[h]], o_c[:])
        for q in range(4):
            eng = nc.sync if q < 2 else nc.scalar
            eng.dma_start(out_2[0][4 * q : 4 * q + 4, :].bitcast(I32), o_s[32 * q : 32 * q + 4, :].bitcast(I32))
